import numpy as np, ml_dtypes
CORES = [2,6,10,14,18,22,26,30]
N = 8
import mx_ref
BF = ml_dtypes.bfloat16
def pick(q, e):
    c = np.concatenate([q[0].reshape(128, -1, 4), np.zeros((128, 1, 4), np.uint8)], axis=1); s = np.concatenate([q[1], np.ones((16, 1), np.uint8)], axis=1)
    return (np.ascontiguousarray(c[:, e].reshape(128, -1)), np.ascontiguousarray(s[:, e]))
def join(*qs):
    return (np.concatenate([q[0] for q in qs], axis=1), np.concatenate([q[1] for q in qs], axis=1))
def put(q, e, v):
    c, s = q[0].reshape(128, -1, 4).copy(), q[1].copy(); c[:, e] = v[0].reshape(128, -1, 4); s[:, e] = v[1]
    return (c.reshape(128, -1), s)
def pk(c, s):
    return (np.ascontiguousarray(c), mx_ref.live(s))
def emit(q):
    return q[0], q[1]
def cols(t, e):
    v = np.concatenate([t.reshape(128, -1, 4), np.zeros((128, 1, 4), BF)], axis=1)
    return np.ascontiguousarray(v[:, e]).reshape(128, -1)
def tile(rs):
    return np.stack(rs, axis=2).reshape(128, -1).astype(BF)
def cut(t, i, w=512):
    return t[:, w * i:w * i + w]
def f(rng, *shape):
    return mx_ref.flush((rng.standard_normal(shape, dtype=np.float32) * np.exp2(rng.integers(-2, 3, shape[:-1] + (1,)))).astype(BF))
def wide(rng, *shape, cols=0):
    v = rng.standard_normal(shape, dtype=np.float32) * np.exp2(rng.integers(-12, 13, shape)).astype(np.float32)
    if cols: v *= np.repeat(np.exp2(rng.integers(-cols, cols + 1, shape[:-2] + (1, shape[-1] // 4))) * (rng.random(shape[:-2] + (1, shape[-1] // 4)) > 0.0625), 4, axis=-1).astype(np.float32)
    return mx_ref.flush(v.astype(BF))
T, CAPP, CB, DF = 128, 32, 16, 64
LEVELS = np.array([0, 16, 32, 64], np.float32)
def taken(first, a):
    return np.concatenate([s * T + np.flatnonzero(first[s] == a)[:CAPP] for s in range(N)])
def plain(rng):
    rt, r2 = np.array(f(rng, 128, 512)), np.zeros((128, 512), BF)
    rt[:, 4 * N:] = 0
    v = f(rng, 128, 4 * N + 4).astype(np.float32).reshape(128, N + 1, 4)
    v = v - np.mean(v, axis=(0, 2), keepdims=True)
    r2[:, :4 * N + 4] = mx_ref.flush(v.reshape(128, -1).astype(BF))
    return {"x": np.array(f(rng, N, 128, 4 * T)), "rt": np.stack([rt] * N), "w": np.array(f(rng, N, 128, 2048)), "r2": np.stack([r2] * N), "vx": f(rng, N, 128, 512), "vh": f(rng, N, 128, 512)}
def planned(rng, A, B, V, dead=None, same=False):
    d = plain(rng)
    rt, r2, wt = d["rt"], d["r2"], d["w"].reshape(N, 128, 4, 128, 4)
    rt[:, 120:] = 0
    r2[:, :4 * N + 4] = 0
    wt[:, 120:] = 0
    for k in range(N + 1):
        r2[:, 4 * k:4 * k + 4, 4 * k:4 * k + 4] = 32
        wt[:, 120 + k // 4, :, 4 * k:4 * k + 4, k % 4] = 64
    k = N + 1
    wt[:, 120 + k // 4, :, :, k % 4] = -64
    if same:
        p = f(rng, 128, 4 * N)
        x = np.stack([cols(p, A[s]) for s in range(N)])
    else: x = f(rng, N, 128, 4 * T)
    x = np.array(x, np.float32).reshape(N, 128, T, 4)
    g = rt[0].astype(np.float32).reshape(128, 128, 4)
    for s in range(N): x[s] = x[s] + g[:, A[s]]
    x[:, 120:] = 0
    s, j = np.nonzero(B >= 0)
    b = B[s, j]
    x[s, 120 + b // 4, j, b % 4] = 64
    x[:, 120 + N // 4, :, N % 4] = LEVELS[V]
    if dead is not None: x[:, 120 + k // 4, :, k % 4] = np.where(dead, 256, 0)
    d["x"] = np.array(mx_ref.flush(x.reshape(N, 128, 4 * T).astype(BF)))
    return d
def choose(rng, A):
    B, V = (A + 1 + rng.integers(0, N - 1, A.shape)) % N, np.zeros((N, T), int)
    for a in range(N):
        k = taken(A, a)
        V.flat[k] = 3
        k = rng.permutation(k)[:DF]
        V.flat[k] = 0
        B.flat[k] = np.resize(rng.permutation([b for b in range(N) if b != a]), len(k))
    return B, V
def setup_inputs(rng):
    return plain(rng)
def setup_inputs_crowd(rng):
    h, A = int(rng.integers(1, N - 1)), []
    o = (int(rng.choice([i for i in range(1, N) if i not in (h, h + 1)])), h)
    for s in range(N):
        one, two, e = (s + o[0]) % N, (s + o[1]) % N, int(rng.integers(1, 9))
        rest = [a for a in range(N) if a not in (one, two, (two + 1) % N)]
        A.append(rng.permutation(np.concatenate([np.full(CAPP, one), np.full(CAPP + e, two), np.resize(rng.permutation(rest), T - 2 * CAPP - e)])))
    A = np.stack(A)
    B, V = choose(rng, A)
    for a in range(N):
        one, two, e = (a + o[0]) % N, (a + o[1]) % N, int(rng.integers(1, CB // 4 + 1))
        rest = [b for b in range(N) if b not in (a, one, two)]
        k = taken(A, a)
        k = rng.permutation(k[V.reshape(-1)[k] == 0])
        B.flat[k] = np.concatenate([np.full(CB, one), np.full(CB + e, two), np.resize(rng.permutation(rest), len(k) - 2 * CB - e)])
    return planned(rng, A, B, V)
def setup_inputs_few(rng):
    none, less, even, full = rng.permutation(N)[:4]
    act, n = [a for a in range(N) if a not in (none, less, even, full)] or [full], DF // (2 * N)
    fix = np.concatenate([np.full(n, less), np.full(2 * n, even), np.full(CAPP + 4, full)])
    A = np.stack([rng.permutation(np.concatenate([fix, np.resize(rng.permutation(act), T - len(fix))])) for s in range(N)])
    B, V = choose(rng, A)
    m = (A == less) | (A == even)
    V[m] = rng.integers(0, 4, int(np.count_nonzero(m)))
    k = taken(A, full)
    V.flat[k] = 3
    k = np.concatenate([k[-16::5], rng.permutation(k[:-16])[:DF - 4]])
    V.flat[k] = 0
    B.flat[k] = np.resize(rng.permutation([b for b in range(N) if b != full]), DF)
    d = planned(rng, A, B, V)
    p, t = 120 + (N + 2) // 4, (N + 2) % 4
    d["x"][:, p, t::4] = 64
    d["w"].reshape(N, 128, 4, 128, 4)[:, p, :, 4 * N + 4:4 * N + 8, t] = 64
    d["r2"][:, 4 * N + 4:4 * N + 8] = 0
    d["r2"][:, 4 * N + 4:4 * N + 8, :4 * N] = -64
    d["x"] = (d["x"].astype(np.float32) * np.float32(2.0 ** 21)).astype(BF)
    d["r2"] = (d["r2"].astype(np.float32) * np.float32(2.0 ** 24)).astype(BF)
    return d
def setup_inputs_ties(rng):
    lo, hi = np.sort(rng.permutation(N)[:2])
    k = int(rng.choice([i for i in range(N - 1) if i != hi]))
    act = [a for a in range(N) if a != hi]
    A = np.stack([rng.permutation(np.resize(rng.permutation(act), T)) for s in range(N)])
    B, V, c = np.zeros((N, T), int), np.full((N, T), 3), 3 * (DF // 6)
    for a in act:
        g = rng.permutation(taken(A, a))
        n = (len(g) - 2 * c) // 3
        B.flat[g] = (a + 1) % N
        V.flat[g[:c]] = 0
        B.flat[g[c:2 * c]] = (a + 2) % N
        V.flat[g[c:2 * c]] = 1
        B.flat[g[2 * c:2 * c + 3 * n]] = (a + 3 + np.repeat(np.arange(n), 3) % (N - 3)) % N
        V.flat[g[2 * c:2 * c + 3 * n]] = 2
    d = planned(rng, A, B, V, same=True)
    d["rt"][:, :, 4 * hi:4 * hi + 4] = d["rt"][:, :, 4 * lo:4 * lo + 4]
    d["r2"][:, 4 * k + 4:4 * k + 8, 4 * k:4 * k + 4] = 32
    d["r2"][:, :, 4 * k + 4:4 * k + 8] = d["r2"][:, :, 4 * k:4 * k + 4]
    return d
def setup_inputs_zero(rng):
    A = np.stack([rng.permutation(np.resize(np.arange(N), T)) for s in range(N)])
    B, V, dead = (A + 1 + rng.integers(0, N - 1, A.shape)) % N, np.full((N, T), 3), np.zeros((N, T), bool)
    for a in range(N):
        k = rng.permutation(taken(A, a))
        z = DF // 2 if a % 2 else DF + DF // 8
        dead.flat[k[:z]] = True
        B.flat[k[:z]] = -1
        V.flat[k[:z]] = 0
        g = k[z:DF]
        if len(g):
            V.flat[g] = 1
            B.flat[g] = np.resize(rng.permutation([b for b in range(N) if b != a]), len(g))
        if a == 0: blank = k[:z:2]
    d = planned(rng, A, B, V, dead=dead)
    nil = np.where(d["rt"][0, :, :4].astype(np.float32) < 0, np.float32(0.0), np.float32(-0.0)).astype(BF)
    for i in blank: d["x"][i // T, :, 4 * (i % T):4 * (i % T) + 4] = nil
    return d
def setup_inputs_spread(rng):
    return {**plain(rng), "x": wide(rng, N, 128, 4 * T, cols=4)}
def check_inputs(d):
    b = []
    for k in ("x", "rt", "w", "r2", "vx", "vh"):
        v = np.abs(d[k].astype(np.float32))
        if not (np.isfinite(v).all() and ((v == 0) | (v >= 2.0 ** -30) & (v <= 2.0 ** 30)).all()): b.append("a value of " + k)
    for k, n in (("rt", N), ("r2", N + 1)):
        v = d[k].astype(np.float32)
        if (v[:, :, 4 * n:] != 0).any(): b.append(k + " has numbers behind its first columns")
        if (v != v[:1]).any(): b.append(k + " differs between ranks")
    return b
def reference(x, rt, w, r2, vx, vh):
    q = [mx_ref.quantize(np.ascontiguousarray(x[s])) for s in range(N)]
    every = join(*q)
    first = np.stack([np.argmax(mx_ref.matmul(mx_ref.quantize(np.ascontiguousarray(rt[s])), q[s])[:N] + np.float32(0.0), axis=0) for s in range(N)])
    who, at, made = np.full((N, N * CB), -1), np.full((N, N * CB), -1), []
    for a in range(N):
        k = taken(first, a)
        t = pick(every, np.concatenate([k, np.full(N * CAPP - len(k), -1)]))
        z = [mx_ref.matmul(mx_ref.quantize(np.ascontiguousarray(cut(w[a], i))), t) for i in range(4)]
        h = mx_ref.quantize(np.ascontiguousarray(tile([np.maximum(v, np.float32(0.0)) * np.float32(0.0625) for v in z])))
        made.append(h)
        e = mx_ref.matmul(mx_ref.quantize(np.ascontiguousarray(r2[a])), h)[:N + 1, :len(k)] + np.float32(0.0)
        late = np.sort(np.argsort(e[N], kind="stable")[:DF])
        e[a] = -np.inf
        second = np.argmax(e[:N], axis=0)
        for b in range(N):
            m = late[second[late] == b][:CB]
            who[b, a * CB:a * CB + len(m)] = k[m]
            at[b, a * CB:a * CB + len(m)] = a * N * CAPP + m
    made = join(*made)
    y, oc, osc = np.zeros((N, 128, N * CB), np.float32), np.zeros((N, 128, 4 * N * CB), np.uint8), np.zeros((N, 16, N * CB), np.uint8)
    for b in range(N):
        t, h = pick(every, who[b]), pick(made, at[b])
        v = mx_ref.matmul(mx_ref.quantize(np.ascontiguousarray(vx[b])), t) + mx_ref.matmul(mx_ref.quantize(np.ascontiguousarray(vh[b])), h)
        y[b] = np.where(who[b] >= 0, v, np.float32(0.0))
        oc[b], osc[b] = emit(h)
    return {"y": y, "who": who.astype(np.float32).reshape(N, 1, N * CB), "oc": oc, "osc": osc}

@@ -1,0 +1,413 @@
+from concourse.bass import DstId, RemoteDMATransfer
+from concourse.mybir import dt, AluOpType as A, AxisListType, ActivationFunctionType as F
+
+N = 8
+TK = 128
+CAPP = 32
+CB = 16
+DF = 64
+SL = N * CAPP
+HO = 384
+XW = 642
+BIG = 2.0 ** 96
+
+SCRATCH = {}
+
+
+def _declare(kind, dtype, **bufs):
+    for name, n in bufs.items():
+        SCRATCH[name] = (kind, n if isinstance(n, list) else [128, n], dtype)
+
+
+_declare("sbuf", "bfloat16", xt=520, rtt=512, wt=2048, r2t=512, r8t=512, vxt=512, vht=512, zt=512, ht=1032)
+_declare("sbuf", "float8_e4m3fn_x4", xq=136, rq=128, wq=512, r2q=128, r8q=128, vxq=128, vhq=128, sq=SL, xh=648, s2q=SL, l2q=SL, hq=128)
+_declare("sbuf", "uint8", xs=136, rs=128, ws=512, r2s=128, r8s=128, vxs=128, vhs=128, ss=SL, xhs=648, s2s=SL, l2s=SL, hs=128)
+_declare("dram", "bfloat16", fd=[128, 1], fl=[N, 128, 1], tokd=[N, 128, 1], tokl=[N, 128, 1])
+_declare("dram", "float32", whod=[N, 128, 1], whol=[N, 128, 1])
+_declare("sbuf", "int32", pp=8, cc=8, ig=8, ih=8, p15=8, p31=8, pb=8)
+_declare("sbuf", "float32", thr1=2, thrh=2, ccol=1, ecol=2, mgt=2, mct=2, mcol=2, neg8=8, lim8=8, io32=32, m1=128)
+_declare("sbuf", "bfloat16", zb=128, rsA=512, c128=32, one=2 * SL, sgn=2 * SL, tokv=144)
+_declare("sbuf", "uint16", offz=2, offh=8, off1=16, off2=16)
+_declare("sbuf", "float32", R=8, first=1, sa=4, lf1=[32, 16], lf2=[32, 8], nb=[32, 1], nbb=[32, 32], nrep=32, nrepb=8, pen=SL,
+         E1=SL, Rm=18, mj=16, mm=2, sg=2, tokw=648, wr=SL, ysb=128)
+_declare("sbuf", "bfloat16", fb=32, fr=128, M1=256, C1=256, L1=512, S1=256, trow=SL, tokr=SL, frl=[32, 128], feq=[32, 128],
+         EQ=2 * SL, FS=2 * SL, SJ=2 * SL, mp=2, fb2=64, fr2=[128, 4, 64], M2=2 * SL, C2=2 * SL, L2=SL, S2=SL)
+_declare("psum", "float32", p0=512, p1=512, p2=512, p3=512, p4=512, p5=512, p6=512, p7=512)
+_DMAS = ["x", "rt", "w", "r2a", "r2b", "vx", "vh", "fd", "fo", "fl", "td", "to", "tl", "wd", "wo", "ti", "wi",
+         "y", "oc", "o0", "o1", "o2", "o3", "who"]
+SEMAPHORES = ["qv", "qa", "qt", "qg", "af", "a1", "at", "a2", "aw", "loc"] + ["d_" + k for k in _DMAS]
+
+
+def plan(T, topo, s):
+    c = T.cores[s]
+    near = [r for r in range(N) if r != s and topo.chip(T.cores[r]) == topo.chip(c)]
+
+    def hops(r):
+        a, b = topo.chip(c), topo.chip(T.cores[r])
+        return 0 if topo.mates(a, b) else 1 if topo.same_plane(a, b) else 2
+    far = sorted([r for r in range(N) if r != s and r not in near], key=lambda r: (hops(r), (r - s) % N))
+    e = topo.engines(c, T.cores[far[0]])
+    k = [x for x in topo.engines(c, T.cores[near[0]]) if x not in e][:2]
+    one = {far[0]: e[0:1], far[1]: e[1:2], far[2]: e[2:3], far[3]: e[3:4], far[4]: e[4:6], far[5]: e[6:8], near[0]: k}
+    two = {far[4]: e[4:5], far[5]: e[5:6], far[0]: e[6:7], far[1]: e[7:8], far[2]: e[0:2], far[3]: e[2:4], near[0]: k}
+    return one, two, {**one, near[0]: e}
+
+
+def rank_program(g, core, T, topo):
+    me = T.rank_of(core)
+    if me is None:
+        return
+    S = T.sem
+    plans = [plan(T, topo, s) for s in range(N)]
+    others = [r for r in range(N) if r != me]
+    far = [r for r in others if topo.chip(T.cores[r]) != topo.chip(core)]
+    near = [r for r in others if r not in far]
+    eng = {"v": g.vector, "a": g.scalar, "t": g.tensor, "s": g.sync, "g": g}
+    vec = g.vector
+    V = {"set": vec.memset, "copy": vec.tensor_copy, "ts": vec.tensor_scalar, "tt": vec.tensor_tensor,
+         "scan": vec.tensor_tensor_scan, "red": vec.tensor_reduce, "tr": vec.transpose, "qz": vec.quantize_mx}
+    G = {"iota": g.iota, "sel": g.affine_select}
+    cnt = {}
+    seen = {q: {} for q in eng}
+    wr, rd = {}, {}
+
+    def need(q, evs):
+        m = {}
+        for sem, n in evs:
+            m[sem] = max(n, m.get(sem, 0))
+        for sem in sorted(m):
+            if seen[q].get(sem, 0) < m[sem]:
+                eng[q].wait_ge(S[sem], m[sem])
+                seen[q][sem] = m[sem]
+
+    def before(q, reads, writes, part):
+        evs = [e for t in reads for e in wr[t]]
+        if not part:
+            evs += [e for t in writes for e in wr.get(t, []) + rd.get(t, [])]
+        need(q, evs)
+
+    def after(ev, reads, writes, part):
+        for t in reads:
+            rd.setdefault(t, []).append(ev)
+        for t in writes:
+            wr[t] = (wr.get(t, []) if part else []) + [ev]
+            if not part:
+                rd[t] = []
+
+    def op(q, f, args, reads=(), writes=(), part=False, **kw):
+        before(q, reads, writes, part)
+        sem = "q" + q
+        cnt[sem] = cnt.get(sem, 0) + 1
+        f(*args, **kw).then_inc(S[sem], 1)
+        after((sem, cnt[sem]), reads, writes, part)
+
+    def v(name, *args, **kw):
+        op("v", V[name], args, **kw)
+
+    def act(*args, **kw):
+        op("a", g.scalar.activation, args, **kw)
+
+    def mm(*args, **kw):
+        op("t", g.tensor.matmul_mx, args, **kw)
+
+    def gp(name, *args, **kw):
+        op("g", G[name], args, **kw)
+
+    def dma(q, key, out, in_, reads=(), writes=(), part=False):
+        before(q, reads, writes, part)
+        eng[q].dma_start(out, in_).then_inc(S["d_" + key], 16)
+        cnt["d_" + key] = 16
+        after(("d_" + key, 16), reads, writes, part)
+
+    def send(to, which, sem, src, dst, reads):
+        need("g", [e for t in reads for e in wr[t]])
+        tr = []
+        for d in to:
+            es = plans[me][which][d]
+            rid, pid, _ = topo.addr(T.cores[d])
+            tr.append(RemoteDMATransfer(dst_ids=[DstId(rid=rid, pnc=pid)], dma_engine_mask=sum(1 << e for e in es),
+                                        remote_sem=S[sem], src=src(d), dst=dst(d)))
+            cnt["loc"] = cnt.get("loc", 0) + len(es)
+        g.remote_dma_fused(tr, local_sem=S["loc"])
+
+    def lands(tag, sem, *which):
+        cnt[sem] = sum(len(plans[s][w][me]) for s in others for w in which)
+        wr[tag].append((sem, cnt[sem]))
+
+    u8, u32 = dt.uint8, dt.uint32
+    blk = [slice(32 * b, 32 * b + 32) for b in range(N)]
+    half = [slice(128 * h, 128 * h + 128) for h in range(4)]
+    row = [slice(SL * h, SL * h + SL) for h in range(2)]
+
+    dma("s", "x", T.xt[:, 0:512], T.x[:, :], writes=["xt"], part=True)
+    dma("a", "rt", T.rtt[:, 0:4 * N], T.rt[:, 0:4 * N], writes=["rtt"], part=True)
+    dma("s", "w", T.wt[:, :], T.w[:, :], writes=["wt"])
+    if me > 0:
+        dma("a", "r2a", T.r2t[:, 0:4 * me], T.r2[:, 0:4 * me], writes=["r2t"], part=True)
+    dma("a", "r2b", T.r2t[:, 4 * me:4 * N], T.r2[:, 4 * me + 4:4 * N + 4], writes=["r2t"], part=True)
+
+    fl = {"allow_small_or_imprecise_dtypes": True}
+    gp("iota", T.pp[:, :], [[0, 8]], 0, 1, writes=["pp"])
+    gp("iota", T.tokv[:, :], [[1, 144]], 0, 0, writes=["tokv"], **fl)
+    gp("iota", T.m1[:, :], [[0, 128]], -1, 0, writes=["m1"], **fl)
+    gp("iota", T.cc[:, :], [[1, 8]], 0, 0, writes=["cc"])
+    gp("iota", T.io32[:, :], [[1, 32]], 0, 0, writes=["io32"], **fl)
+    v("set", T.zb[:, :], 0.0, writes=["zb"])
+    v("set", T.rtt[:, 4 * N:512], 0.0, writes=["rtt"], part=True)
+    v("set", T.xt[:, 512:520], 0.0, writes=["xt"], part=True)
+    v("set", T.neg8[:, :], -9e29, writes=["neg8"])
+    v("ts", T.pb[:, :], T.pp[:, :], 4, 14, A.logical_shift_right, A.bitwise_and, reads=["pp"], writes=["pb"])
+    v("ts", T.p15[:, :], T.pp[:, :], 15, None, A.bitwise_and, reads=["pp"], writes=["p15"])
+    for u in range(2):
+        v("ts", T.ecol[:, u:u + 1], T.pb[:, 0:1], float(u), None, A.add, reads=["pb"], writes=["ecol"], part=True)
+        v("ts", T.thr1[:, u:u + 1], T.p15[:, 0:1], 16.0 * u, None, A.add, reads=["p15"], writes=["thr1"], part=True)
+    for k in range(4):
+        act(T.rsA[:, half[k]], T.zb[:, :], F.Identity, reads=["zb"], writes=["rsA1"], part=True, bias=1.0)
+    act(T.rsA[:, 0:512:128], T.zb[:, 0:4], F.Copy, reads=["zb", "rsA1"], writes=["rsA"])
+    act(T.thrh[:, :], T.thr1[:, :], F.Identity, reads=["thr1"], writes=["thrh"], bias=0.5)
+    dma("a", "wo", T.whol[me:me + 1, 0:CB, 0], T.m1[0:1, 0:CB], reads=["m1"], writes=["whol"], part=True)
+    dma("a", "wi", T.whod[:, :, 0], T.m1[0:N, :], reads=["m1"], writes=["whod"])
+    dma("a", "ti", T.tokd[:, :, 0], T.zb[0:N, :], reads=["zb"], writes=["tokd"])
+
+    v("qz", T.rq[:, :], T.rs[:, :], T.rtt[:, :], reads=["rtt"], writes=["rq"])
+    v("qz", T.xq[:, 0:130], T.xs[:, 0:130], T.xt[:, :], reads=["xt"], writes=["xq"])
+    mm(T.p0[:, 0:128], T.xq[:, 0:128], T.xs[:, 0:128], T.rq[:, :], T.rs[:, :], True, True, reads=["xq", "rq"], writes=["p0"])
+    v("scan", T.R[:, :], T.p0[:, 0:8], T.neg8[:, :], -9e29, A.max, A.max, reads=["p0", "neg8"], writes=["R"])
+    act(T.mj[:, 0:8], T.R[:, :], F.Sign, reads=["R"], writes=["first"], bias=T.R[:, 7:8], scale=-1.0, accum_out=T.first[:, 0:1])
+    v("ts", T.fb[:, :], T.zb[:, 0:32], T.first[:, 0:1], None, A.add, reads=["zb", "first"], writes=["fb"])
+    dma("s", "fd", T.fd[:, :], T.fb[:, 0:1], reads=["fb"], writes=["fd"])
+    dma("s", "fo", T.fl[me], T.fb[:, 0:1], reads=["fb"], writes=["fl"], part=True)
+    send(near, 2, "af", lambda d: T.fb[:, 0:1], lambda d: T.fl[me], ["fb"])
+    for a in range(4):
+        v("tr", T.fr[0:32, blk[a]], T.fb[blk[a], :], reads=["fb"], writes=["fr"], part=True)
+    act(T.fr[blk[3], :], T.fr[0:32, :], F.Copy, reads=["fr"], writes=["frc"])
+    for b in range(1, 3):
+        v("copy", T.fr[blk[b], :], T.fr[0:32, :], reads=["fr"], writes=["fra"], part=b > 1)
+    for u in range(2):
+        v("ts", T.M1[:, half[u]], T.fr[:, :], T.ecol[:, u:u + 1], None, A.is_equal,
+          reads=["fr", "fra", "frc", "ecol"], writes=["M1%d" % u])
+    for u in range(2):
+        v("scan", T.C1[:, half[u]], T.rsA[:, half[u]], T.M1[:, half[u]], 0.0, A.mult, A.add, reads=["rsA", "M1%d" % u], writes=["C1%d" % u])
+    for h in range(2):
+        act(T.L1[:, half[2 + h]], T.C1[:, half[0]], F.Sign, reads=["C10", "thrh"], writes=["sa"], part=True,
+            bias=T.thrh[:, h:h + 1], scale=-1.0, accum_out=T.sa[:, h:h + 1])
+        v("ts", T.L1[:, half[h]], T.C1[:, half[1]], T.thr1[:, h:h + 1], None, A.is_le, reads=["C11", "thr1"], writes=["L1%d" % h])
+    for h in range(2):
+        v("scan", T.S1[:, half[h]], T.rsA[:, half[h]], T.L1[:, half[h]], 0.0, A.mult, A.add, reads=["rsA", "L1%d" % h], writes=["S1"], part=True)
+    for b in range(4):
+        act(T.lf1[0:32, 4 * b:4 * b + 2], T.sa[blk[b], 0:2], F.Identity, reads=["sa"], writes=["lf1"], part=True, bias=64.0, scale=0.5)
+        v("copy", T.lf1[0:32, 4 * b + 2:4 * b + 4], T.S1[blk[b], 127:256:128], reads=["S1"], writes=["lf1"], part=True)
+    for b in range(4):
+        v("copy", T.off1[blk[b], :], T.lf1[0:32, :], reads=["lf1"], writes=["off1"], part=True)
+    O1 = ["off1", "xq"]
+    ms = slice(2 * me, 2 * me + 2)
+    v("copy", T.sq[:, :].bitcast(u32), T.xq[:, 0:130].bitcast(u32).indirect(T.off1[:, :]), reads=O1, writes=["sq"])
+    act(T.ss[:, :], T.xs[:, 0:130].indirect(T.off1[:, :]), F.Copy, reads=O1, writes=["ss"])
+    v("copy", T.xh[:, blk[me]].bitcast(u32), T.xq[:, 0:130].bitcast(u32).indirect(T.off1[:, ms]), reads=O1, writes=["xh"], part=True)
+    act(T.xhs[:, blk[me]], T.xs[:, 0:130].indirect(T.off1[:, ms]), F.Copy, reads=O1, writes=["xh"], part=True)
+    act(T.trow[:, :], T.tokv[:, :].indirect(T.off1[:, :]), F.Copy, reads=O1 + ["tokv"], writes=["trow"])
+
+    send(far, 2, "af", lambda d: T.fd[:, :], lambda d: T.fl[me], ["fd"])
+    send(others, 0, "a1", lambda d: T.sq[:, blk[d]].bitcast(u8), lambda d: T.xh[:, blk[me]].bitcast(u8), ["sq"])
+    send(others, 1, "a1", lambda d: T.ss[:, blk[d]], lambda d: T.xhs[:, blk[me]], ["ss"])
+    lands("fl", "af", 2)
+    dma("s", "fl", T.frl[0:8, :], T.fl[:, :, 0], reads=["fl"], writes=["frl"])
+    dma("s", "td", T.tokd[:, 0:CAPP, 0], T.trow[0:1, :], reads=["trow"], writes=["tokd"])
+    dma("s", "to", T.tokl[me:me + 1, 0:CAPP, 0], T.trow[0:1, blk[me]], reads=["trow"], writes=["tokl"], part=True)
+
+    act(T.sgn[:, :], T.wt[:, 0:2 * SL], F.Identity, reads=["wt"], writes=["sgn1"], bias=1.0, scale=0.0)
+    for t in range(4):
+        act(T.r8t[:, t:512:4], T.zb[:, :], F.Identity, reads=["r2t", "zb"], writes=["r8t"], part=True, bias=T.r2t[:, 28 + t:29 + t])
+    act(T.one[:, :], T.wt[:, 0:2 * SL], F.Identity, reads=["wt"], writes=["one1"], bias=1.0, scale=0.0)
+    act(T.tokw[:, :], T.wt[:, 0:648], F.Identity, reads=["wt"], writes=["tokm"], bias=-1.0, scale=0.0)
+    v("qz", T.wq[:, :], T.ws[:, :], T.wt[:, :], reads=["wt"], writes=["wq"])
+    v("set", T.zt[:, :], 0.0, writes=["zt"])
+    v("set", T.r2t[:, 4 * N:512], 0.0, writes=["r2z"])
+    v("set", T.ht[:, 1024:1032], 0.0, writes=["htz"])
+    v("copy", T.offz[:, :], T.thr1[:, :], reads=["thr1"], writes=["offz"])
+    v("qz", T.xh[:, 256:384], T.xhs[:, 256:384], T.zt[:, :], reads=["zt"], writes=["xhz"])
+    v("qz", T.r2q[:, :], T.r2s[:, :], T.r2t[:, :], reads=["r2t", "r2z"], writes=["r2q"])
+    v("ts", T.p31[:, :], T.pp[:, :], 31, None, A.bitwise_and, reads=["pp"], writes=["p31"])
+    v("set", T.nb[:, :], 0.0, writes=["nb"])
+    v("qz", T.r8q[:, :], T.r8s[:, :], T.r8t[:, :], reads=["r8t"], writes=["r8q"])
+    v("copy", T.ccol[:, :], T.p31[:, 0:1], reads=["p31"], writes=["ccol"])
+    OZ = ["offz", "xhz"]
+    v("copy", T.l2q[:, blk[me]].bitcast(u32), T.xh[:, 256:384].bitcast(u32).indirect(T.offz[:, :]), reads=OZ, writes=["l2"], part=True)
+    v("copy", T.l2s[:, blk[me]], T.xhs[:, 256:384].indirect(T.offz[:, :]), reads=OZ, writes=["l2"], part=True)
+    v("ts", T.ig[:, :], T.cc[:, :], 32.0, float(CB), A.mult, A.add, reads=["cc"], writes=["ig"])
+    v("ts", T.mgt[:, :], T.ecol[:, :], float(me), -1.0, A.is_gt, A.mult, reads=["ecol"], writes=["mgt"])
+    v("tt", T.ih[:, :], T.ig[:, :], T.p15[:, :], A.add, reads=["ig", "p15"], writes=["ih"])
+    v("tt", T.mct[:, :], T.ecol[:, :], T.mgt[:, :], A.add, reads=["ecol", "mgt"], writes=["mct"])
+    v("copy", T.offh[:, :], T.ih[:, :], reads=["ih"], writes=["offh"])
+    v("ts", T.mcol[:, :], T.mct[:, :], 1.0, None, A.add, reads=["mct"], writes=["mcol"])
+    v("set", T.lim8[:, 0:7], 9e29, writes=["lim8"], part=True)
+    v("set", T.lim8[:, 7:8], -9e29, writes=["lim8"], part=True)
+    v("set", T.c128[:, :], 128.0, writes=["c128"])
+    v("set", T.one[:, 0:2 * SL:SL], 0.0, reads=["one1"], writes=["one"])
+    for h in range(2):
+        k = slice(SL * h + 128 * h, SL * h + 128 * h + 128)
+        gp("sel", T.sgn[:, k], T.sgn[:, k], [[-1, 128]], A.not_equal, -1.0, 0, 1, reads=["sgn1"], writes=["sgn"], part=True)
+    send(others, 0, "at", lambda d: T.tokd[d], lambda d: T.tokl[me], ["tokd"])
+
+    v("ts", T.feq[0:8, :], T.frl[0:8, :], float(me), None, A.is_equal, reads=["frl"], writes=["feq"])
+    red(v, T.nb[0:8, :], T.feq[0:8, :], reads=["feq"], writes=["nb"])
+    v("ts", T.nbb[:, :], T.zb[0:32, 0:32], T.nb[:, 0:1], None, A.add, reads=["zb", "nb"], writes=["nbb"])
+    v("tr", T.nrep[0:32, :], T.nbb[:, :], reads=["nbb"], writes=["nrep"])
+    for b in range(1, 4):
+        v("copy", T.nrep[blk[b], :], T.nrep[0:32, :], reads=["nrep"], writes=["nrepa"], part=True)
+    NR = ["nrep", "nrepa"]
+
+    def pens(*ranks):
+        for s in ranks:
+            v("ts", T.pen[:, blk[s]], T.io32[:, :], T.nrep[:, s:s + 1], BIG, A.is_ge, A.mult,
+              reads=NR + ["io32"], writes=["pen%d" % (s // 4)], part=True)
+
+    def nbs():
+        act(T.nrepb[:, :], T.nrep[:, 0:8], F.Identity, reads=NR, writes=["nrepb"], bias=BIG, scale=-BIG)
+
+    def pns(*ranks):
+        for s in ranks:
+            act(T.pen[:, blk[s]], T.io32[:, :], F.Relu, reads=["nrepb", "io32"], writes=["pen%d" % (s // 4)], part=True,
+                bias=T.nrepb[:, s:s + 1], scale=BIG)
+
+    def pcs(*blocks):
+        for a in blocks:
+            v("ts", T.Rm[blk[a], 0:18:9], T.nrep[blk[a], a:8:4], T.ccol[blk[a], 0:1], -9e29, A.is_gt, A.mult,
+              reads=NR + ["ccol"], writes=["Rmc"], part=True)
+    fill = {(0, 0): [(nbs,), (pns, 4)], (0, 2): [(pns, 5)], (1, 0): [(pns, 6, 7)],
+            (0, 1): [(pens, 0, 1)], (0, 3): [(pens, 2)], (1, 1): [(pens, 3), (pcs, 0)], (1, 3): [(pcs, 1)], (1, 4): [(pcs, 2, 3)]}
+    lands("tokl", "at", 0)
+    dma("s", "tl", T.tokr[0:1, :], T.tokl[:, 0:CAPP, 0], reads=["tokl"], writes=["tokr"])
+    dma("s", "vx", T.vxt[:, :], T.vx[:, :], writes=["vxt"])
+    dma("s", "vh", T.vht[:, :], T.vh[:, :], writes=["vht"])
+
+    lands("xh", "a1", 0, 1)
+    P = [[T.p1, T.p2, T.p3, T.p4], [T.p0, T.p5, T.p6, T.p7]]
+    B = [["p1", "p2", "p3", "p4"], ["p0", "p5", "p6", "p7"]]
+    for h in range(2):
+        for i in range(4):
+            mm(P[h][i][:, 0:128], T.wq[:, half[i]], T.ws[:, half[i]], T.xh[:, half[h]], T.xhs[:, half[h]], True, True,
+               reads=["wq", "xh"], writes=[B[h][i]])
+    ROW, rw, PE, pe = [T.p1, T.p4], ["p1", "p4"], [T.p2, T.p3], ["p2", "p3"]
+
+    def products(h):
+        k = slice(HO + 128 * h, HO + 128 * h + 128)
+        mm(ROW[h][:, 0:128], T.r8q[:, :], T.r8s[:, :], T.xh[:, k], T.xhs[:, k], True, True, reads=["r8q", "h%d" % h], writes=[rw[h]])
+        mm(PE[h][:, 0:128], T.xh[:, k], T.xhs[:, k], T.r2q[:, :], T.r2s[:, :], True, True, reads=["r2q", "h%d" % h], writes=[pe[h]])
+    for h in range(2):
+        e = 512 * (h + 1)
+        for i in range(4):
+            o = T.ht[:, 512 * h + i:e:4]
+            if i % 2:
+                v("ts", o, P[h][i][:, 0:128], 0.0, 0.0625, A.max, A.mult, reads=[B[h][i]], writes=["ht%d" % h], part=True)
+            else:
+                act(o, P[h][i][:, 0:128], F.Relu, reads=[B[h][i]], writes=["ht%d" % h], part=True, scale=0.0625)
+            for f, *n in fill.get((h, i), []):
+                f(*n)
+        k = slice(HO + 128 * h, XW if h else HO + 128)
+        v("qz", T.xh[:, k], T.xhs[:, k], T.ht[:, 512 * h:e + 8 * h], reads=["ht%d" % h, "htz"], writes=["h%d" % h])
+        products(h)
+        for f, *n in fill.get((h, 4), []):
+            f(*n)
+
+    def second(h):
+        k = 9 * h
+        v("scan", T.Rm[:, k + 1:k + 9], T.lim8[:, :], PE[h][:, 0:8], -9e29, A.min, A.max, reads=[pe[h], "lim8"], writes=["Rm%d" % h])
+
+    def away(h):
+        v("tt", T.E1[:, half[h]], ROW[h][:, 0:128], T.pen[:, half[h]], A.add, reads=[rw[h], "pen%d" % h], writes=["E1"], part=True)
+    second(0)
+    away(0)
+    away(1)
+    second(1)
+
+    def number(h):
+        k = 9 * h
+        act(T.mj[:, 8 * h:8 * h + 8], T.Rm[:, k:k + 8], F.Sign, reads=["Rm%d" % h, "Rmc"], writes=["mm%d" % h],
+            bias=T.Rm[:, k + 7:k + 8], scale=-1.0, accum_out=T.mm[:, h:h + 1])
+        act(T.mp[:, h:h + 1], T.mm[:, h:h + 1], F.Copy, reads=["mm%d" % h], writes=["mp%d" % h])
+    number(0)
+    for h in range(2):
+        e8 = T.Rm[:, 9 * h + 8:9 * h + 9]
+        act(T.SJ[:, row[h]], T.E1[:, :], F.Sign, reads=["E1", "Rm%d" % h], writes=["sg%d" % h],
+            bias=e8, scale=-1.0, accum_out=T.sg[:, h:h + 1])
+        v("ts", T.EQ[:, row[h]], T.E1[:, :], e8, None, A.is_equal, reads=["E1", "Rm%d" % h], writes=["EQ%d" % h])
+    number(1)
+
+    def rank(h):
+        v("scan", T.FS[:, row[h]], T.sgn[:, row[h]], T.EQ[:, row[h]], T.sg[:, h:h + 1], A.mult, A.add,
+          reads=["sgn", "EQ%d" % h, "sg%d" % h], writes=["FS%d" % h])
+    rank(0)
+    rank(1)
+    for h in range(2):
+        v("ts", T.fb2[:, blk[h]], T.c128[:, :], T.FS[:, SL * h + SL - 1:SL * h + SL], T.mp[:, h:h + 1], A.is_lt, A.mult,
+          reads=["c128", "FS%d" % h, "mp%d" % h], writes=["fb2"], part=True)
+    for a in range(4):
+        v("tr", T.fr2[0:32, a, :], T.fb2[blk[a], :], reads=["fb2"], writes=["fr2"], part=True)
+    act(T.fr2[blk[3], :, :], T.fr2[0:32, :, :], F.Copy, reads=["fr2"], writes=["fr2c"])
+    for b in range(1, 3):
+        v("copy", T.fr2[blk[b], :, :], T.fr2[0:32, :, :], reads=["fr2"], writes=["fr2a"], part=b > 1)
+    for u in range(2):
+        for h in range(2):
+            v("ts", T.M2[:, half[2 * u + h]], T.fr2[:, :, blk[h]], T.mcol[:, u:u + 1], None, A.is_equal,
+              reads=["fr2", "fr2a", "fr2c", "mcol"], writes=["M2%d" % u], part=True)
+    for u in range(2):
+        v("scan", T.C2[:, row[u]], T.one[:, row[u]], T.M2[:, row[u]], 0.0, A.mult, A.add, reads=["one", "M2%d" % u], writes=["C2%d" % u])
+    act(T.SJ[:, row[0]], T.C2[:, row[0]], F.Sign, reads=["C20", "thrh"], writes=["sa2"],
+        bias=T.thrh[:, 0:1], scale=-1.0, accum_out=T.sa[:, 2:3])
+    for h in range(2):
+        v("ts", T.L2[:, half[h]], T.C2[:, half[2 + h]], T.thr1[:, 0:1], None, A.is_le, reads=["C21", "thr1"], writes=["L2%d" % h])
+    for h in range(2):
+        v("scan", T.S2[:, half[h]], T.one[:, half[h]], T.L2[:, half[h]], 0.0, A.mult, A.add, reads=["one", "L2%d" % h], writes=["S2"], part=True)
+    for b in range(4):
+        act(T.lf2[0:32, 2 * b:2 * b + 1], T.sa[blk[b], 2:3], F.Identity, reads=["sa2"], writes=["lf2"], part=True, bias=128.0, scale=0.5)
+        v("tt", T.lf2[0:32, 2 * b + 1:2 * b + 2], T.S2[blk[b], 127:128], T.S2[blk[b], 255:256], A.add, reads=["S2"], writes=["lf2"], part=True)
+    for s in range(N):
+        act(T.tokw[0:1, blk[s]], T.tokr[0:1, blk[s]], F.Identity, reads=["tokr", "tokm"], writes=["tokw"], part=True, bias=float(TK * s))
+    for b in range(4):
+        v("copy", T.off2[blk[b], 0:16:2], T.lf2[0:32, :], reads=["lf2"], writes=["off2%d" % (b // 2)], part=True)
+    for k in range(2):
+        q = slice(64 * k, 64 * k + 64)
+        v("ts", T.off2[q, 1:16:2], T.off2[q, 0:16:2], float(HO), None, A.add, reads=["off2%d" % k], writes=["off2a"], part=True)
+    O2 = ["off20", "off21", "off2a"]
+    XR = O2 + ["xh", "xhz", "h0", "h1"]
+    v("copy", T.s2q[:, :].bitcast(u32), T.xh[:, 0:XW].bitcast(u32).indirect(T.off2[:, :]), reads=XR, writes=["s2q"])
+    act(T.wr[:, :], T.tokw[:, 0:XW].indirect(T.off2[:, :]), F.Copy, reads=O2 + ["tokw", "tokm"], writes=["wr"])
+    act(T.s2s[:, :], T.xhs[:, 0:XW].indirect(T.off2[:, :]), F.Copy, reads=XR, writes=["s2s"])
+    send(others, 0, "a2", lambda d: T.s2q[:, blk[d]].bitcast(u8), lambda d: T.l2q[:, blk[me]].bitcast(u8), ["s2q"])
+    send(others, 1, "a2", lambda d: T.s2s[:, blk[d]], lambda d: T.l2s[:, blk[me]], ["s2s"])
+
+    dma("s", "wd", T.whod[:, 0:2 * CB, 0], T.wr[0:1, :], reads=["wr"], writes=["whod"])
+    send(others, 0, "aw", lambda d: T.whod[d], lambda d: T.whol[me], ["whod"])
+    v("qz", T.vxq[:, :], T.vxs[:, :], T.vxt[:, :], reads=["vxt"], writes=["vxq"])
+    v("qz", T.vhq[:, :], T.vhs[:, :], T.vht[:, :], reads=["vht"], writes=["vhq"])
+
+    lands("l2", "a2", 0, 1)
+    Y, yt = [T.p0, T.p5], ["p0", "p5"]
+    for q in range(2):
+        n, t = (144, 128)[q], yt[q]
+        k, j = slice(112 * q, 112 * q + n), slice(112 * q + CB, 112 * q + CB + n)
+        mm(Y[q][:, 0:n], T.vxq[:, :], T.vxs[:, :], T.l2q[:, k], T.l2s[:, k], True, False, reads=["vxq", "l2"], writes=[t])
+        mm(Y[q][:, 0:n], T.vhq[:, :], T.vhs[:, :], T.l2q[:, j], T.l2s[:, j], False, True, reads=["vhq", "l2"], writes=[t], part=True)
+    v("copy", T.hq[:, :].bitcast(u32), T.l2q[:, :].bitcast(u32).indirect(T.offh[:, :]), reads=["l2", "offh"], writes=["hq"])
+    act(T.hs[:, :], T.l2s[:, :].indirect(T.offh[:, :]), F.Copy, reads=["l2", "offh"], writes=["hs"])
+    for a in range(N):
+        k = 32 * a - 112 * (a // 5)
+        o, i = T.ysb[:, CB * a:CB * a + CB], Y[a // 5][:, k:k + CB]
+        if a < 5:
+            v("copy", o, i, reads=[yt[0]], writes=["ysb"], part=True)
+        else:
+            act(o, i, F.Copy, reads=[yt[1]], writes=["ysb"], part=True)
+    dma("s", "oc", T.oc[:, :], T.hq[:, :].bitcast(u8), reads=["hq"], writes=["oc"])
+    for k in range(4):
+        dma("s" if k < 2 else "a", "o%d" % k, T.osc[4 * k:4 * k + 4, :], T.hs[32 * k:32 * k + 4, :], reads=["hs"], writes=["osc%d" % k])
+    dma("s", "y", T.y[:, :], T.ysb[:, :], reads=["ysb"], writes=["y"])
+    lands("whol", "aw", 0)
+    dma("s", "who", T.who[0:1, :], T.whol[:, 0:CB, 0], reads=["whol"], writes=["who"])
+    for sem in sorted(cnt):
+        if max(seen[q].get(sem, 0) for q in eng) < cnt[sem]:
+            need("a" if sem in ("d_o2", "d_o3") else "s" if sem[:2] == "d_" else "g", [(sem, cnt[sem])])
+
+
+def red(v, out, in_, **kw):
+    v("red", out, in_, axis=AxisListType.X, op=A.add, **kw)

@@ -1,5 +1,5 @@
 from concourse.bass import DstId, RemoteDMATransfer
-from concourse.mybir import dt, AluOpType as A, AxisListType, ActivationFunctionType as F
+from concourse.mybir import dt, AluOpType as A, ActivationFunctionType as F
 
 N = 8
 TK = 128
@@ -10,6 +10,7 @@ SL = N * CAPP
 HO = 384
 XW = 642
 BIG = 2.0 ** 96
+K = 256.0
 
 SCRATCH = {}
 
@@ -25,13 +26,13 @@ _declare("sbuf", "uint8", xs=136, rs=128, ws=512, r2s=128, r8s=128, vxs=128, vhs
 _declare("dram", "bfloat16", fd=[128, 1], fl=[N, 128, 1], tokd=[N, 128, 1], tokl=[N, 128, 1])
 _declare("dram", "float32", whod=[N, 128, 1], whol=[N, 128, 1])
 _declare("sbuf", "int32", pp=8, cc=8, ig=8, ih=8, p15=8, p31=8, pb=8)
-_declare("sbuf", "float32", thr1=2, thrh=2, ccol=1, ecol=2, mgt=2, mct=2, mcol=2, neg8=8, lim8=8, io32=32, m1=128)
-_declare("sbuf", "bfloat16", zb=128, rsA=512, c128=32, one=2 * SL, sgn=2 * SL, tokv=144)
+_declare("sbuf", "float32", thk=2, ccol=1, ecol=2, mgt=2, mct=2, mcol=2, neg8=8, lim8=8, hoc=4, m1=128)
+_declare("sbuf", "bfloat16", zb=SL, c128=32, keep=SL, sgn=2 * SL, tokv=SL + 2)
 _declare("sbuf", "uint16", offz=2, offh=8, off1=16, off2=16)
-_declare("sbuf", "float32", R=8, first=1, sa=4, lf1=[32, 16], lf2=[32, 8], nb=[32, 1], nbb=[32, 32], nrep=32, nrepb=8, pen=SL,
-         E1=SL, Rm=18, mj=16, mm=2, sg=2, tokw=648, wr=SL, ysb=128)
-_declare("sbuf", "bfloat16", fb=32, fr=128, M1=256, C1=256, L1=512, S1=256, trow=SL, tokr=SL, frl=[32, 128], feq=[32, 128],
-         EQ=2 * SL, FS=2 * SL, SJ=2 * SL, mp=2, fb2=64, fr2=[128, 4, 64], M2=2 * SL, C2=2 * SL, L2=SL, S2=SL)
+_declare("sbuf", "float32", R=8, first=1, sa=2, lf1=[32, 16], lf2=[32, 16], E1=SL, Rm=18, mj=16, mm=2, sg=2, tokw=648, wr=SL, ysb=128)
+_declare("sbuf", "bfloat16", fb=32, fr=128, M1=256, D1=384, L1=256, S1=256, trow=SL, tokr=SL, frl=[32, 128], feq=[32, 128],
+         ns=[32, 160], nt=[32, 32], pd=SL, pen=SL, EQ=2 * SL, FS=2 * SL, SJ=2 * SL, mp=2, fb2=64, fr2=[128, 4, 64], M2=2 * SL,
+         D2=[128, 2, SL + 2], S2=[128, 2, SL + 2])
 _declare("psum", "float32", p0=512, p1=512, p2=512, p3=512, p4=512, p5=512, p6=512, p7=512)
 _DMAS = ["x", "rt", "w", "r2a", "r2b", "vx", "vh", "fd", "fo", "fl", "td", "to", "tl", "wd", "wo", "ti", "wi",
          "y", "oc", "o0", "o1", "o2", "o3", "who"]
@@ -65,8 +66,8 @@ def rank_program(g, core, T, topo):
     eng = {"v": g.vector, "a": g.scalar, "t": g.tensor, "s": g.sync, "g": g}
     vec = g.vector
     V = {"set": vec.memset, "copy": vec.tensor_copy, "ts": vec.tensor_scalar, "tt": vec.tensor_tensor,
-         "scan": vec.tensor_tensor_scan, "red": vec.tensor_reduce, "tr": vec.transpose, "qz": vec.quantize_mx}
-    G = {"iota": g.iota, "sel": g.affine_select}
+         "scan": vec.tensor_tensor_scan, "tr": vec.transpose, "qz": vec.quantize_mx}
+    G = {"iota": g.iota, "sel": g.affine_select, "all": g.partition_broadcast}
     cnt = {}
     seen = {q: {} for q in eng}
     wr, rd = {}, {}
@@ -148,26 +149,21 @@ def rank_program(g, core, T, topo):
 
     fl = {"allow_small_or_imprecise_dtypes": True}
     gp("iota", T.pp[:, :], [[0, 8]], 0, 1, writes=["pp"])
-    gp("iota", T.tokv[:, :], [[1, 144]], 0, 0, writes=["tokv"], **fl)
-    gp("iota", T.m1[:, :], [[0, 128]], -1, 0, writes=["m1"], **fl)
+    gp("iota", T.tokv[:, :], [[1, SL + 2]], 0, 0, writes=["tokv"], **fl)
     gp("iota", T.cc[:, :], [[1, 8]], 0, 0, writes=["cc"])
-    gp("iota", T.io32[:, :], [[1, 32]], 0, 0, writes=["io32"], **fl)
     v("set", T.zb[:, :], 0.0, writes=["zb"])
     v("set", T.rtt[:, 4 * N:512], 0.0, writes=["rtt"], part=True)
     v("set", T.xt[:, 512:520], 0.0, writes=["xt"], part=True)
     v("set", T.neg8[:, :], -9e29, writes=["neg8"])
+    v("set", T.m1[:, :], -1.0, writes=["m1"])
     v("ts", T.pb[:, :], T.pp[:, :], 4, 14, A.logical_shift_right, A.bitwise_and, reads=["pp"], writes=["pb"])
     v("ts", T.p15[:, :], T.pp[:, :], 15, None, A.bitwise_and, reads=["pp"], writes=["p15"])
     for u in range(2):
         v("ts", T.ecol[:, u:u + 1], T.pb[:, 0:1], float(u), None, A.add, reads=["pb"], writes=["ecol"], part=True)
-        v("ts", T.thr1[:, u:u + 1], T.p15[:, 0:1], 16.0 * u, None, A.add, reads=["p15"], writes=["thr1"], part=True)
-    for k in range(4):
-        act(T.rsA[:, half[k]], T.zb[:, :], F.Identity, reads=["zb"], writes=["rsA1"], part=True, bias=1.0)
-    act(T.rsA[:, 0:512:128], T.zb[:, 0:4], F.Copy, reads=["zb", "rsA1"], writes=["rsA"])
-    act(T.thrh[:, :], T.thr1[:, :], F.Identity, reads=["thr1"], writes=["thrh"], bias=0.5)
+        v("ts", T.thk[:, u:u + 1], T.p15[:, 0:1], 16.0 * u + 1.0, K, A.add, A.mult, reads=["p15"], writes=["thk"], part=True)
     dma("a", "wo", T.whol[me:me + 1, 0:CB, 0], T.m1[0:1, 0:CB], reads=["m1"], writes=["whol"], part=True)
     dma("a", "wi", T.whod[:, :, 0], T.m1[0:N, :], reads=["m1"], writes=["whod"])
-    dma("a", "ti", T.tokd[:, :, 0], T.zb[0:N, :], reads=["zb"], writes=["tokd"])
+    dma("a", "ti", T.tokd[:, :, 0], T.zb[0:N, 0:128], reads=["zb"], writes=["tokd"])
 
     v("qz", T.rq[:, :], T.rs[:, :], T.rtt[:, :], reads=["rtt"], writes=["rq"])
     v("qz", T.xq[:, 0:130], T.xs[:, 0:130], T.xt[:, :], reads=["xt"], writes=["xq"])
@@ -184,16 +180,16 @@ def rank_program(g, core, T, topo):
     for b in range(1, 3):
         v("copy", T.fr[blk[b], :], T.fr[0:32, :], reads=["fr"], writes=["fra"], part=b > 1)
     for u in range(2):
-        v("ts", T.M1[:, half[u]], T.fr[:, :], T.ecol[:, u:u + 1], None, A.is_equal,
+        v("ts", T.M1[:, half[u]], T.fr[:, :], T.ecol[:, u:u + 1], -K, A.is_equal, A.mult,
           reads=["fr", "fra", "frc", "ecol"], writes=["M1%d" % u])
-    for u in range(2):
-        v("scan", T.C1[:, half[u]], T.rsA[:, half[u]], T.M1[:, half[u]], 0.0, A.mult, A.add, reads=["rsA", "M1%d" % u], writes=["C1%d" % u])
+    for k, (u, h) in enumerate([(0, 0), (1, 0), (1, 1)]):
+        v("scan", T.D1[:, half[k]], T.M1[:, half[u]], T.zb[:, 0:128], T.thk[:, h:h + 1], A.add, A.add,
+          reads=["zb", "thk", "M1%d" % u], writes=["D1%d" % k])
     for h in range(2):
-        act(T.L1[:, half[2 + h]], T.C1[:, half[0]], F.Sign, reads=["C10", "thrh"], writes=["sa"], part=True,
-            bias=T.thrh[:, h:h + 1], scale=-1.0, accum_out=T.sa[:, h:h + 1])
-        v("ts", T.L1[:, half[h]], T.C1[:, half[1]], T.thr1[:, h:h + 1], None, A.is_le, reads=["C11", "thr1"], writes=["L1%d" % h])
-    for h in range(2):
-        v("scan", T.S1[:, half[h]], T.rsA[:, half[h]], T.L1[:, half[h]], 0.0, A.mult, A.add, reads=["rsA", "L1%d" % h], writes=["S1"], part=True)
+        act(T.L1[:, half[h]], T.D1[:, half[0]], F.Sign, reads=["D10"], writes=["sa"], part=True,
+            bias=K * (16 * h - 0.5), accum_out=T.sa[:, h:h + 1])
+        v("scan", T.S1[:, half[h]], T.D1[:, half[1 + h]], T.tokv[:, 1:129], 0.0, A.max, A.min,
+          reads=["tokv", "D1%d" % (1 + h)], writes=["S1"], part=True)
     for b in range(4):
         act(T.lf1[0:32, 4 * b:4 * b + 2], T.sa[blk[b], 0:2], F.Identity, reads=["sa"], writes=["lf1"], part=True, bias=64.0, scale=0.5)
         v("copy", T.lf1[0:32, 4 * b + 2:4 * b + 4], T.S1[blk[b], 127:256:128], reads=["S1"], writes=["lf1"], part=True)
@@ -202,35 +198,37 @@ def rank_program(g, core, T, topo):
     O1 = ["off1", "xq"]
     ms = slice(2 * me, 2 * me + 2)
     v("copy", T.sq[:, :].bitcast(u32), T.xq[:, 0:130].bitcast(u32).indirect(T.off1[:, :]), reads=O1, writes=["sq"])
+    act(T.trow[:, :], T.tokv[:, 0:144].indirect(T.off1[:, :]), F.Copy, reads=O1 + ["tokv"], writes=["trow"])
     act(T.ss[:, :], T.xs[:, 0:130].indirect(T.off1[:, :]), F.Copy, reads=O1, writes=["ss"])
     v("copy", T.xh[:, blk[me]].bitcast(u32), T.xq[:, 0:130].bitcast(u32).indirect(T.off1[:, ms]), reads=O1, writes=["xh"], part=True)
-    act(T.xhs[:, blk[me]], T.xs[:, 0:130].indirect(T.off1[:, ms]), F.Copy, reads=O1, writes=["xh"], part=True)
-    act(T.trow[:, :], T.tokv[:, :].indirect(T.off1[:, :]), F.Copy, reads=O1 + ["tokv"], writes=["trow"])
+    v("copy", T.xhs[:, blk[me]], T.xs[:, 0:130].indirect(T.off1[:, ms]), reads=O1, writes=["xh"], part=True)
 
     send(far, 2, "af", lambda d: T.fd[:, :], lambda d: T.fl[me], ["fd"])
     send(others, 0, "a1", lambda d: T.sq[:, blk[d]].bitcast(u8), lambda d: T.xh[:, blk[me]].bitcast(u8), ["sq"])
     send(others, 1, "a1", lambda d: T.ss[:, blk[d]], lambda d: T.xhs[:, blk[me]], ["ss"])
-    lands("fl", "af", 2)
-    dma("s", "fl", T.frl[0:8, :], T.fl[:, :, 0], reads=["fl"], writes=["frl"])
     dma("s", "td", T.tokd[:, 0:CAPP, 0], T.trow[0:1, :], reads=["trow"], writes=["tokd"])
     dma("s", "to", T.tokl[me:me + 1, 0:CAPP, 0], T.trow[0:1, blk[me]], reads=["trow"], writes=["tokl"], part=True)
+    lands("fl", "af", 2)
+    dma("s", "fl", T.frl[0:8, :], T.fl[:, :, 0], reads=["fl"], writes=["frl"])
+    send(others, 0, "at", lambda d: T.tokd[d], lambda d: T.tokl[me], ["tokd"])
 
     act(T.sgn[:, :], T.wt[:, 0:2 * SL], F.Identity, reads=["wt"], writes=["sgn1"], bias=1.0, scale=0.0)
     for t in range(4):
-        act(T.r8t[:, t:512:4], T.zb[:, :], F.Identity, reads=["r2t", "zb"], writes=["r8t"], part=True, bias=T.r2t[:, 28 + t:29 + t])
-    act(T.one[:, :], T.wt[:, 0:2 * SL], F.Identity, reads=["wt"], writes=["one1"], bias=1.0, scale=0.0)
+        act(T.r8t[:, t:512:4], T.zb[:, 0:128], F.Identity, reads=["r2t", "zb"], writes=["r8t"], part=True, bias=T.r2t[:, 28 + t:29 + t])
+    act(T.keep[:, :], T.zb[:, :], F.Identity, reads=["zb"], writes=["keep1"], bias=1.0)
+    act(T.pd[:, :], T.zb[:, :], F.Identity, reads=["zb"], writes=["pd1"], bias=BIG)
     act(T.tokw[:, :], T.wt[:, 0:648], F.Identity, reads=["wt"], writes=["tokm"], bias=-1.0, scale=0.0)
     v("qz", T.wq[:, :], T.ws[:, :], T.wt[:, :], reads=["wt"], writes=["wq"])
     v("set", T.zt[:, :], 0.0, writes=["zt"])
     v("set", T.r2t[:, 4 * N:512], 0.0, writes=["r2z"])
     v("set", T.ht[:, 1024:1032], 0.0, writes=["htz"])
-    v("copy", T.offz[:, :], T.thr1[:, :], reads=["thr1"], writes=["offz"])
+    v("set", T.offz[:, :], 0, writes=["offz"])
     v("qz", T.xh[:, 256:384], T.xhs[:, 256:384], T.zt[:, :], reads=["zt"], writes=["xhz"])
     v("qz", T.r2q[:, :], T.r2s[:, :], T.r2t[:, :], reads=["r2t", "r2z"], writes=["r2q"])
     v("ts", T.p31[:, :], T.pp[:, :], 31, None, A.bitwise_and, reads=["pp"], writes=["p31"])
-    v("set", T.nb[:, :], 0.0, writes=["nb"])
+    v("set", T.ns[:, :], 0.0, writes=["ns"])
     v("qz", T.r8q[:, :], T.r8s[:, :], T.r8t[:, :], reads=["r8t"], writes=["r8q"])
-    v("copy", T.ccol[:, :], T.p31[:, 0:1], reads=["p31"], writes=["ccol"])
+    v("ts", T.ccol[:, :], T.p31[:, 0:1], BIG, None, A.mult, reads=["p31"], writes=["ccol"])
     OZ = ["offz", "xhz"]
     v("copy", T.l2q[:, blk[me]].bitcast(u32), T.xh[:, 256:384].bitcast(u32).indirect(T.offz[:, :]), reads=OZ, writes=["l2"], part=True)
     v("copy", T.l2s[:, blk[me]], T.xhs[:, 256:384].indirect(T.offz[:, :]), reads=OZ, writes=["l2"], part=True)
@@ -243,39 +241,25 @@ def rank_program(g, core, T, topo):
     v("set", T.lim8[:, 0:7], 9e29, writes=["lim8"], part=True)
     v("set", T.lim8[:, 7:8], -9e29, writes=["lim8"], part=True)
     v("set", T.c128[:, :], 128.0, writes=["c128"])
-    v("set", T.one[:, 0:2 * SL:SL], 0.0, reads=["one1"], writes=["one"])
+    v("set", T.keep[:, 0:SL:CAPP], 0.0, reads=["keep1"], writes=["keep"])
+    v("set", T.D2[:, :, SL:SL + 2], 0.0, writes=["D2z"])
+    v("set", T.hoc[:, 0:4:2], 0.0, writes=["hoc"], part=True)
+    v("set", T.hoc[:, 1:4:2], float(HO), writes=["hoc"], part=True)
     for h in range(2):
         k = slice(SL * h + 128 * h, SL * h + 128 * h + 128)
         gp("sel", T.sgn[:, k], T.sgn[:, k], [[-1, 128]], A.not_equal, -1.0, 0, 1, reads=["sgn1"], writes=["sgn"], part=True)
-    send(others, 0, "at", lambda d: T.tokd[d], lambda d: T.tokl[me], ["tokd"])
 
-    v("ts", T.feq[0:8, :], T.frl[0:8, :], float(me), None, A.is_equal, reads=["frl"], writes=["feq"])
-    red(v, T.nb[0:8, :], T.feq[0:8, :], reads=["feq"], writes=["nb"])
-    v("ts", T.nbb[:, :], T.zb[0:32, 0:32], T.nb[:, 0:1], None, A.add, reads=["zb", "nb"], writes=["nbb"])
-    v("tr", T.nrep[0:32, :], T.nbb[:, :], reads=["nbb"], writes=["nrep"])
-    for b in range(1, 4):
-        v("copy", T.nrep[blk[b], :], T.nrep[0:32, :], reads=["nrep"], writes=["nrepa"], part=True)
-    NR = ["nrep", "nrepa"]
+    v("ts", T.feq[0:8, :], T.frl[0:8, :], float(me), -BIG, A.is_equal, A.mult, reads=["frl"], writes=["feq"])
+    v("scan", T.ns[0:8, 0:128], T.feq[0:8, :], T.zb[0:8, 0:128], 0.5 * BIG, A.add, A.add, reads=["feq", "zb"], writes=["ns"])
+    v("tr", T.nt[:, :], T.ns[:, 127:159], reads=["ns"], writes=["nt"])
+    gp("all", T.pd[:, 0:SL:CAPP], T.nt[0:1, 0:N], 128, reads=["nt", "pd1"], writes=["pd"])
 
-    def pens(*ranks):
-        for s in ranks:
-            v("ts", T.pen[:, blk[s]], T.io32[:, :], T.nrep[:, s:s + 1], BIG, A.is_ge, A.mult,
-              reads=NR + ["io32"], writes=["pen%d" % (s // 4)], part=True)
+    def pens(h):
+        v("scan", T.pen[:, half[h]], T.keep[:, half[h]], T.pd[:, half[h]], 0.0, A.mult, A.add, reads=["keep", "pd"], writes=["pen%d" % h])
 
-    def nbs():
-        act(T.nrepb[:, :], T.nrep[:, 0:8], F.Identity, reads=NR, writes=["nrepb"], bias=BIG, scale=-BIG)
-
-    def pns(*ranks):
-        for s in ranks:
-            act(T.pen[:, blk[s]], T.io32[:, :], F.Relu, reads=["nrepb", "io32"], writes=["pen%d" % (s // 4)], part=True,
-                bias=T.nrepb[:, s:s + 1], scale=BIG)
-
-    def pcs(*blocks):
-        for a in blocks:
-            v("ts", T.Rm[blk[a], 0:18:9], T.nrep[blk[a], a:8:4], T.ccol[blk[a], 0:1], -9e29, A.is_gt, A.mult,
-              reads=NR + ["ccol"], writes=["Rmc"], part=True)
-    fill = {(0, 0): [(nbs,), (pns, 4)], (0, 2): [(pns, 5)], (1, 0): [(pns, 6, 7)],
-            (0, 1): [(pens, 0, 1)], (0, 3): [(pens, 2)], (1, 1): [(pens, 3), (pcs, 0)], (1, 3): [(pcs, 1)], (1, 4): [(pcs, 2, 3)]}
+    def pcs(a):
+        act(T.Rm[blk[a], 0:18:9], T.pd[blk[a], 32 * a:SL:128], F.Identity, reads=["pd", "ccol"], writes=["Rmc"], part=True,
+            bias=T.ccol[blk[a], 0:1])
     lands("tokl", "at", 0)
     dma("s", "tl", T.tokr[0:1, :], T.tokl[:, 0:CAPP, 0], reads=["tokl"], writes=["tokr"])
     dma("s", "vx", T.vxt[:, :], T.vx[:, :], writes=["vxt"])
@@ -294,30 +278,33 @@ def rank_program(g, core, T, topo):
         k = slice(HO + 128 * h, HO + 128 * h + 128)
         mm(ROW[h][:, 0:128], T.r8q[:, :], T.r8s[:, :], T.xh[:, k], T.xhs[:, k], True, True, reads=["r8q", "h%d" % h], writes=[rw[h]])
         mm(PE[h][:, 0:128], T.xh[:, k], T.xhs[:, k], T.r2q[:, :], T.r2s[:, :], True, True, reads=["r2q", "h%d" % h], writes=[pe[h]])
+
+    def cast(q, h, i):
+        o = T.ht[:, 512 * h + i:512 * (h + 1):4]
+        if q == "v":
+            v("ts", o, P[h][i][:, 0:128], 0.0, 0.0625, A.max, A.mult, reads=[B[h][i]], writes=["ht%d" % h], part=True)
+        else:
+            act(o, P[h][i][:, 0:128], F.Relu, reads=[B[h][i]], writes=["ht%d" % h], part=True, scale=0.0625)
     for h in range(2):
-        e = 512 * (h + 1)
         for i in range(4):
-            o = T.ht[:, 512 * h + i:e:4]
-            if i % 2:
-                v("ts", o, P[h][i][:, 0:128], 0.0, 0.0625, A.max, A.mult, reads=[B[h][i]], writes=["ht%d" % h], part=True)
-            else:
-                act(o, P[h][i][:, 0:128], F.Relu, reads=[B[h][i]], writes=["ht%d" % h], part=True, scale=0.0625)
-            for f, *n in fill.get((h, i), []):
-                f(*n)
+            cast(("avav", "aaav")[h][i], h, i)
+        if h:
+            pens(0)
         k = slice(HO + 128 * h, XW if h else HO + 128)
-        v("qz", T.xh[:, k], T.xhs[:, k], T.ht[:, 512 * h:e + 8 * h], reads=["ht%d" % h, "htz"], writes=["h%d" % h])
+        v("qz", T.xh[:, k], T.xhs[:, k], T.ht[:, 512 * h:512 * (h + 1) + 8 * h], reads=["ht%d" % h, "htz"], writes=["h%d" % h])
         products(h)
-        for f, *n in fill.get((h, 4), []):
-            f(*n)
+    for a in range(4):
+        pcs(a)
 
     def second(h):
         k = 9 * h
         v("scan", T.Rm[:, k + 1:k + 9], T.lim8[:, :], PE[h][:, 0:8], -9e29, A.min, A.max, reads=[pe[h], "lim8"], writes=["Rm%d" % h])
 
     def away(h):
-        v("tt", T.E1[:, half[h]], ROW[h][:, 0:128], T.pen[:, half[h]], A.add, reads=[rw[h], "pen%d" % h], writes=["E1"], part=True)
-    second(0)
+        v("tt", T.E1[:, half[h]], ROW[h][:, 0:128], T.pen[:, half[h]], A.max, reads=[rw[h], "pen%d" % h], writes=["E1"], part=True)
+    pens(1)
     away(0)
+    second(0)
     away(1)
     second(1)
 
@@ -349,27 +336,23 @@ def rank_program(g, core, T, topo):
         v("copy", T.fr2[blk[b], :, :], T.fr2[0:32, :, :], reads=["fr2"], writes=["fr2a"], part=b > 1)
     for u in range(2):
         for h in range(2):
-            v("ts", T.M2[:, half[2 * u + h]], T.fr2[:, :, blk[h]], T.mcol[:, u:u + 1], None, A.is_equal,
+            v("ts", T.M2[:, half[2 * u + h]], T.fr2[:, :, blk[h]], T.mcol[:, u:u + 1], -K, A.is_equal, A.mult,
               reads=["fr2", "fr2a", "fr2c", "mcol"], writes=["M2%d" % u], part=True)
-    for u in range(2):
-        v("scan", T.C2[:, row[u]], T.one[:, row[u]], T.M2[:, row[u]], 0.0, A.mult, A.add, reads=["one", "M2%d" % u], writes=["C2%d" % u])
-    act(T.SJ[:, row[0]], T.C2[:, row[0]], F.Sign, reads=["C20", "thrh"], writes=["sa2"],
-        bias=T.thrh[:, 0:1], scale=-1.0, accum_out=T.sa[:, 2:3])
-    for h in range(2):
-        v("ts", T.L2[:, half[h]], T.C2[:, half[2 + h]], T.thr1[:, 0:1], None, A.is_le, reads=["C21", "thr1"], writes=["L2%d" % h])
-    for h in range(2):
-        v("scan", T.S2[:, half[h]], T.one[:, half[h]], T.L2[:, half[h]], 0.0, A.mult, A.add, reads=["one", "L2%d" % h], writes=["S2"], part=True)
-    for b in range(4):
-        act(T.lf2[0:32, 2 * b:2 * b + 1], T.sa[blk[b], 2:3], F.Identity, reads=["sa2"], writes=["lf2"], part=True, bias=128.0, scale=0.5)
-        v("tt", T.lf2[0:32, 2 * b + 1:2 * b + 2], T.S2[blk[b], 127:128], T.S2[blk[b], 255:256], A.add, reads=["S2"], writes=["lf2"], part=True)
     for s in range(N):
         act(T.tokw[0:1, blk[s]], T.tokr[0:1, blk[s]], F.Identity, reads=["tokr", "tokm"], writes=["tokw"], part=True, bias=float(TK * s))
+    for u in range(2):
+        v("scan", T.D2[:, u, 0:SL], T.M2[:, row[u]], T.zb[:, :], T.thk[:, 0:1], A.add, A.add, reads=["zb", "thk", "M2%d" % u], writes=["D2%d" % u])
+    for u in range(2):
+        v("scan", T.S2[:, u, 0:SL + 1], T.D2[:, u, 0:SL + 1], T.tokv[:, 1:SL + 2], 0.0, A.max, A.min,
+          reads=["tokv", "D2z", "D2%d" % u], writes=["S2"], part=True)
+    for b in range(3):
+        v("tt", T.lf2[0:32, 4 * b:4 * b + 4], T.S2[blk[b], :, SL - 1:SL + 1], T.hoc[blk[b], :], A.add, reads=["S2", "hoc"], writes=["lf2"], part=True)
+    for u in range(2):
+        act(T.lf2[0:32, 12 + 2 * u:14 + 2 * u], T.hoc[blk[3], 0:2], F.Identity, reads=["S2", "hoc"], writes=["lf2"], part=True,
+            bias=T.S2[blk[3], u, SL:SL + 1])
     for b in range(4):
-        v("copy", T.off2[blk[b], 0:16:2], T.lf2[0:32, :], reads=["lf2"], writes=["off2%d" % (b // 2)], part=True)
-    for k in range(2):
-        q = slice(64 * k, 64 * k + 64)
-        v("ts", T.off2[q, 1:16:2], T.off2[q, 0:16:2], float(HO), None, A.add, reads=["off2%d" % k], writes=["off2a"], part=True)
-    O2 = ["off20", "off21", "off2a"]
+        v("copy", T.off2[blk[b], :], T.lf2[0:32, :], reads=["lf2"], writes=["off2"], part=True)
+    O2 = ["off2"]
     XR = O2 + ["xh", "xhz", "h0", "h1"]
     v("copy", T.s2q[:, :].bitcast(u32), T.xh[:, 0:XW].bitcast(u32).indirect(T.off2[:, :]), reads=XR, writes=["s2q"])
     act(T.wr[:, :], T.tokw[:, 0:XW].indirect(T.off2[:, :]), F.Copy, reads=O2 + ["tokw", "tokm"], writes=["wr"])
@@ -407,7 +390,3 @@ def rank_program(g, core, T, topo):
     for sem in sorted(cnt):
         if max(seen[q].get(sem, 0) for q in eng) < cnt[sem]:
             need("a" if sem in ("d_o2", "d_o3") else "s" if sem[:2] == "d_" else "g", [(sem, cnt[sem])])
-
-
-def red(v, out, in_, **kw):
-    v("red", out, in_, axis=AxisListType.X, op=A.add, **kw)

@@ -5,12 +5,14 @@ N = 8
 TK = 128
 CAPP = 32
 CB = 16
-DF = 64
 SL = N * CAPP
+OUT = SL - CAPP
 HO = 384
 XW = 642
 BIG = 2.0 ** 96
 K = 256.0
+CALLS1 = "q4 q5 s6 s7"
+CALLS2 = "q0 s0 s1 q1"
 
 SCRATCH = {}
 
@@ -20,23 +22,23 @@ def _declare(kind, dtype, **bufs):
         SCRATCH[name] = (kind, n if isinstance(n, list) else [128, n], dtype)
 
 
-_declare("sbuf", "bfloat16", xt=520, rtt=512, wt=2048, r2t=512, r8t=512, vxt=512, vht=512, zt=512, ht=1032)
-_declare("sbuf", "float8_e4m3fn_x4", xq=136, rq=128, wq=512, r2q=128, r8q=128, vxq=128, vhq=128, sq=SL, xh=648, s2q=SL, l2q=SL, hq=128)
-_declare("sbuf", "uint8", xs=136, rs=128, ws=512, r2s=128, r8s=128, vxs=128, vhs=128, ss=SL, xhs=648, s2s=SL, l2s=SL, hs=128)
+_declare("sbuf", "bfloat16", xt=520, rtt=512, wt=2048, r2t=512, r8t=512, vxt=512, vht=512, ht=1032)
+_declare("sbuf", "float8_e4m3fn_x4", xq=136, rq=128, wq=512, r2q=128, r8q=128, vxq=128, vhq=128, sq=OUT, xh=648, s2q=OUT, l2q=SL, hq=128)
+_declare("sbuf", "uint8", xs=136, rs=128, ws=512, r2s=128, r8s=128, vxs=128, vhs=128, ss=OUT, xhs=648, s2s=OUT, l2s=SL, hs=128)
 _declare("dram", "bfloat16", fd=[128, 1], fl=[N, 128, 1], tokd=[N, 128, 1], tokl=[N, 128, 1])
 _declare("dram", "float32", whod=[N, 128, 1], whol=[N, 128, 1])
-_declare("sbuf", "int32", pp=8, cc=8, ig=8, ih=8, p15=8, p31=8, pb=8)
-_declare("sbuf", "float32", thk=2, ccol=1, ecol=2, mgt=2, mct=2, mcol=2, neg8=8, lim8=8, hoc=4, m1=128)
-_declare("sbuf", "bfloat16", zb=SL, c128=32, keep=SL, sgn=2 * SL, tokv=SL + 2)
-_declare("sbuf", "uint16", offz=2, offh=8, off1=16, off2=16)
-_declare("sbuf", "float32", R=8, first=1, sa=2, lf1=[32, 16], lf2=[32, 16], E1=SL, Rm=18, mj=16, mm=2, sg=2, tokw=648, wr=SL, ysb=128)
-_declare("sbuf", "bfloat16", fb=32, fr=128, M1=256, D1=384, L1=256, S1=256, trow=SL, tokr=SL, frl=[32, 128], feq=[32, 128],
-         ns=[32, 160], nt=[32, 32], pd=SL, pen=SL, EQ=2 * SL, FS=2 * SL, SJ=2 * SL, mp=2, fb2=64, fr2=[128, 4, 64], M2=2 * SL,
-         D2=[128, 2, SL + 2], S2=[128, 2, SL + 2])
+_declare("sbuf", "int32", pp=8, p15=8, p31=8)
+_declare("sbuf", "float32", thk=3, ccol=1, ecol=2, mlt=2, mcol=2, neg8=8, lim8=8, hoc=4, m1=128)
+_declare("sbuf", "bfloat16", zb=SL, c128=32, keep=SL, sgn=384, tokv=SL + 2, two=128)
+_declare("sbuf", "uint16", offz=2, offh=8, offw=8, off1=16, off2=14)
+_declare("sbuf", "float32", R=8, first=1, Z1=512, lf1=[32, 16], lf2=[32, 16], E1=SL, Rm=18, mj=16, mm=2, sg=2, tokw=SL + 2, wr=128, ysb=128)
+_declare("sbuf", "bfloat16", fb=32, fr=128, M1=256, D1=384, L1=256, trow=SL, tokr=SL, frl=[32, 128], feq=[32, 128],
+         ns=[32, 160], nt=[32, 32], pd=SL, pen=SL, EQ=2 * SL, FS=2 * SL, SJ=2 * SL, mp=2, fb2=64, fr2=[128, 2, 128],
+         M2=[128, 4, 128], D2=[128, 2, SL + 2], S2=[128, 2, SL + 2])
 _declare("psum", "float32", p0=512, p1=512, p2=512, p3=512, p4=512, p5=512, p6=512, p7=512)
-_DMAS = ["x", "rt", "w", "r2a", "r2b", "vx", "vh", "fd", "fo", "fl", "td", "to", "tl", "wd", "wo", "ti", "wi",
+_DMAS = ["x", "rt", "w", "w2", "r2a", "r2b", "vx", "vh", "fd", "fo", "fl", "td", "to", "tl", "wd", "wo", "ti", "wi",
          "y", "oc", "o0", "o1", "o2", "o3", "who"]
-SEMAPHORES = ["qv", "qa", "qt", "qg", "af", "a1", "at", "a2", "aw", "loc"] + ["d_" + k for k in _DMAS]
+SEMAPHORES = ["qv", "qa", "qt", "qg", "af", "a10", "a11", "at", "a20", "a21", "a2s", "aw", "loc"] + ["d_" + k for k in _DMAS]
 
 
 def plan(T, topo, s):
@@ -46,12 +48,16 @@ def plan(T, topo, s):
     def hops(r):
         a, b = topo.chip(c), topo.chip(T.cores[r])
         return 0 if topo.mates(a, b) else 1 if topo.same_plane(a, b) else 2
-    far = sorted([r for r in range(N) if r != s and r not in near], key=lambda r: (hops(r), (r - s) % N))
+    far = sorted([r for r in range(N) if r != s and r not in near], key=lambda r: (hops(r), topo.die(T.cores[r]) == topo.die(c)))
     e = topo.engines(c, T.cores[far[0]])
-    k = [x for x in topo.engines(c, T.cores[near[0]]) if x not in e][:2]
-    one = {far[0]: e[0:1], far[1]: e[1:2], far[2]: e[2:3], far[3]: e[3:4], far[4]: e[4:6], far[5]: e[6:8], near[0]: k}
-    two = {far[4]: e[4:5], far[5]: e[5:6], far[0]: e[6:7], far[1]: e[7:8], far[2]: e[0:2], far[3]: e[2:4], near[0]: k}
-    return one, two, {**one, near[0]: e}
+    k = [x for x in topo.engines(c, T.cores[near[0]]) if x not in e][0:4:2]
+    four = {far[0]: e[0:2], far[2]: e[2:4], far[4]: e[4:6], far[5]: e[6:8]}
+    two = {far[1]: e[0:4], far[3]: e[4:8]}
+    short = {**{d: [x] for d, x in zip(far, e)}, near[0]: k[:1]}
+    firsts = {**{d: [e[1 + 4 * (i % 2)]] for i, d in enumerate(far)}, near[0]: e}
+    switch = {far[2]: e[0:2], far[4]: e[2:4], far[3]: e[4:6], far[5]: e[6:8], near[0]: k}
+    mates = {far[0]: e[0:4], far[1]: e[4:8]}
+    return {**four, near[0]: k}, two, short, firsts, four, {near[0]: k, **two}, switch, mates
 
 
 def rank_program(g, core, T, topo):
@@ -63,12 +69,16 @@ def rank_program(g, core, T, topo):
     others = [r for r in range(N) if r != me]
     far = [r for r in others if topo.chip(T.cores[r]) != topo.chip(core)]
     near = [r for r in others if r not in far]
+    order = list(plans[me][0]) + list(plans[me][1]) + [me]
+    n1 = len(plans[me][0])
+    hs = [1 - me // 4, me // 4]
+    come = [[s for s in range(N) if d in plans[s][0]] + [d] + [s for s in range(N) if d in plans[s][1]] for d in range(N)]
     eng = {"v": g.vector, "a": g.scalar, "t": g.tensor, "s": g.sync, "g": g}
     vec = g.vector
     V = {"set": vec.memset, "copy": vec.tensor_copy, "ts": vec.tensor_scalar, "tt": vec.tensor_tensor,
          "scan": vec.tensor_tensor_scan, "tr": vec.transpose, "qz": vec.quantize_mx}
     G = {"iota": g.iota, "sel": g.affine_select, "all": g.partition_broadcast}
-    cnt = {}
+    cnt, queue = {}, {}
     seen = {q: {} for q in eng}
     wr, rd = {}, {}
 
@@ -108,6 +118,9 @@ def rank_program(g, core, T, topo):
     def act(*args, **kw):
         op("a", g.scalar.activation, args, **kw)
 
+    def const(out, src, tag, c, name, part=False):
+        act(out, src, F.Identity, reads=[tag], writes=[name], part=part, bias=float(c), scale=0.0)
+
     def mm(*args, **kw):
         op("t", g.tensor.matmul_mx, args, **kw)
 
@@ -117,53 +130,79 @@ def rank_program(g, core, T, topo):
     def dma(q, key, out, in_, reads=(), writes=(), part=False):
         before(q, reads, writes, part)
         eng[q].dma_start(out, in_).then_inc(S["d_" + key], 16)
-        cnt["d_" + key] = 16
+        cnt["d_" + key], queue["d_" + key] = 16, q
         after(("d_" + key, 16), reads, writes, part)
 
     def send(to, which, sem, src, dst, reads):
+        def name(r):
+            return sem + str(hs.index(r // 4)) if sem == "a1" else sem
         need("g", [e for t in reads for e in wr[t]])
         tr = []
-        for d in to:
-            es = plans[me][which][d]
-            rid, pid, _ = topo.addr(T.cores[d])
-            tr.append(RemoteDMATransfer(dst_ids=[DstId(rid=rid, pnc=pid)], dma_engine_mask=sum(1 << e for e in es),
-                                        remote_sem=S[sem], src=src(d), dst=dst(d)))
+        for es in sorted({tuple(plans[me][which][d]) for d in to}):
+            ds = [d for d in to if tuple(plans[me][which][d]) == es]
+            ad = [topo.addr(T.cores[d]) for d in ds]
+            tr.append(RemoteDMATransfer(dst_ids=[DstId(rid=a[0], pnc=a[1]) for a in ad], dma_engine_mask=sum(1 << e for e in es),
+                                        remote_sem=S[name(ds[0])], srcs=[src(ds[0])], dsts=[dst(d) for d in ds]))
             cnt["loc"] = cnt.get("loc", 0) + len(es)
         g.remote_dma_fused(tr, local_sem=S["loc"])
+        for s in to:
+            cnt[name(s)] = cnt.get(name(s), 0) + len(plans[s][which][me])
 
-    def lands(tag, sem, *which):
-        cnt[sem] = sum(len(plans[s][w][me]) for s in others for w in which)
-        wr[tag].append((sem, cnt[sem]))
+    def lands(tag, sem):
+        wr.setdefault(tag, []).append((sem, cnt[sem]))
 
     u8, u32 = dt.uint8, dt.uint32
     blk = [slice(32 * b, 32 * b + 32) for b in range(N)]
     half = [slice(128 * h, 128 * h + 128) for h in range(4)]
     row = [slice(SL * h, SL * h + SL) for h in range(2)]
+    cols = {st: [slice(0, 32 * n), slice(32 * n, OUT)] for st, n in ((1, n1 - 1), (2, n1))}
+    offs = {st: [slice(0, 2 * n), slice(2 * n, 14)] for st, n in ((1, n1 - 1), (2, n1))}
+
+    def columns(q, s, lq, ls, at, calls, tags, sems):
+        for (kind, w), tag, sem in zip(calls.split(), tags, sems):
+            w = int(w)
+            if kind == "q":
+                send(list(plans[me][w]), w, sem, lambda d: q[:, blk[order.index(d)]].bitcast(u8), lambda d: lq[:, at(d)].bitcast(u8), [tag])
+            else:
+                send(list(plans[me][w]), w, sem, lambda d: s[:, blk[order.index(d)]], lambda d: ls[:, at(d)], [tag])
 
     dma("s", "x", T.xt[:, 0:512], T.x[:, :], writes=["xt"], part=True)
     dma("a", "rt", T.rtt[:, 0:4 * N], T.rt[:, 0:4 * N], writes=["rtt"], part=True)
-    dma("s", "w", T.wt[:, :], T.w[:, :], writes=["wt"])
+    dma("s", "w", T.wt[:, 0:1024], T.w[:, 0:1024], writes=["wt"], part=True)
     if me > 0:
-        dma("a", "r2a", T.r2t[:, 0:4 * me], T.r2[:, 0:4 * me], writes=["r2t"], part=True)
-    dma("a", "r2b", T.r2t[:, 4 * me:4 * N], T.r2[:, 4 * me + 4:4 * N + 4], writes=["r2t"], part=True)
+        dma("s", "r2a", T.r2t[:, 0:4 * me], T.r2[:, 0:4 * me], writes=["r2t"], part=True)
+    dma("s", "r2b", T.r2t[:, 4 * me:4 * N], T.r2[:, 4 * me + 4:4 * N + 4], writes=["r2t"], part=True)
 
     fl = {"allow_small_or_imprecise_dtypes": True}
     gp("iota", T.pp[:, :], [[0, 8]], 0, 1, writes=["pp"])
     gp("iota", T.tokv[:, :], [[1, SL + 2]], 0, 0, writes=["tokv"], **fl)
-    gp("iota", T.cc[:, :], [[1, 8]], 0, 0, writes=["cc"])
     v("set", T.zb[:, :], 0.0, writes=["zb"])
     v("set", T.rtt[:, 4 * N:512], 0.0, writes=["rtt"], part=True)
     v("set", T.xt[:, 512:520], 0.0, writes=["xt"], part=True)
     v("set", T.neg8[:, :], -9e29, writes=["neg8"])
-    v("set", T.m1[:, :], -1.0, writes=["m1"])
-    v("ts", T.pb[:, :], T.pp[:, :], 4, 14, A.logical_shift_right, A.bitwise_and, reads=["pp"], writes=["pb"])
     v("ts", T.p15[:, :], T.pp[:, :], 15, None, A.bitwise_and, reads=["pp"], writes=["p15"])
-    for u in range(2):
-        v("ts", T.ecol[:, u:u + 1], T.pb[:, 0:1], float(u), None, A.add, reads=["pb"], writes=["ecol"], part=True)
-        v("ts", T.thk[:, u:u + 1], T.p15[:, 0:1], 16.0 * u + 1.0, K, A.add, A.mult, reads=["p15"], writes=["thk"], part=True)
-    dma("a", "wo", T.whol[me:me + 1, 0:CB, 0], T.m1[0:1, 0:CB], reads=["m1"], writes=["whol"], part=True)
-    dma("a", "wi", T.whod[:, :, 0], T.m1[0:N, :], reads=["m1"], writes=["whod"])
-    dma("a", "ti", T.tokd[:, :, 0], T.zb[0:N, 0:128], reads=["zb"], writes=["tokd"])
+    v("ts", T.p31[:, :], T.pp[:, :], 31, None, A.bitwise_and, reads=["pp"], writes=["p31"])
+    v("set", T.offz[:, :], TK, writes=["offz"])
+    for u in range(3):
+        v("ts", T.thk[:, u:u + 1], T.p15[:, 0:1], (0.5, 16.5, 1.0)[u], K, A.add, A.mult, reads=["p15"], writes=["thk"], part=True)
+    v("ts", T.ccol[:, :], T.p31[:, 0:1], BIG, None, A.mult, reads=["p31"], writes=["ccol"])
+    v("set", T.offw[:, :], 0, writes=["offw"])
+    const(T.m1[:, :], T.zb[:, 0:128], "zb", -1, "m1")
+    const(T.sgn[:, 0:SL], T.zb[:, :], "zb", 1, "sgn1", True)
+    const(T.sgn[:, SL:384], T.zb[:, 0:128], "zb", 1, "sgn1", True)
+    gp("sel", T.sgn[:, half[1]], T.sgn[:, half[1]], [[-1, 128]], A.not_equal, -1.0, 0, 1, reads=["sgn1"], writes=["sgn"])
+    dma("s", "ti", T.tokd[:, :, 0], T.zb[0:N, 0:128], reads=["zb"], writes=["tokd"])
+    dma("s", "wo", T.whol[me:me + 1, 0:CB, 0], T.m1[0:1, 0:CB], reads=["m1"], writes=["whol"], part=True)
+    dma("s", "wi", T.whod[:, :, 0], T.m1[0:N, :], reads=["m1"], writes=["whod"])
+    act(T.two[:, :], T.tokv[:, 1:129], F.Identity, reads=["tokv"], writes=["two"], bias=-128.0, scale=2.0)
+    for b in range(4):
+        e0, e1 = order[2 * b], order[2 * b + 1]
+        act(T.ecol[blk[b], :], T.tokv[blk[b], 0:2], F.Identity, reads=["tokv"], writes=["ecol"], part=True, bias=float(e0), scale=float(e1 - e0))
+    const(T.lim8[:, 0:7], T.zb[:, 0:7], "zb", 9e29, "lim8", True)
+    const(T.lim8[:, 7:8], T.zb[:, 0:1], "zb", -9e29, "lim8", True)
+    const(T.c128[:, :], T.zb[:, 0:32], "zb", 128, "c128")
+    const(T.hoc[:, 0:4:2], T.zb[:, 0:2], "zb", 0, "hoc", True)
+    const(T.hoc[:, 1:4:2], T.zb[:, 0:2], "zb", HO, "hoc", True)
 
     v("qz", T.rq[:, :], T.rs[:, :], T.rtt[:, :], reads=["rtt"], writes=["rq"])
     v("qz", T.xq[:, 0:130], T.xs[:, 0:130], T.xt[:, :], reads=["xt"], writes=["xq"])
@@ -173,7 +212,8 @@ def rank_program(g, core, T, topo):
     v("ts", T.fb[:, :], T.zb[:, 0:32], T.first[:, 0:1], None, A.add, reads=["zb", "first"], writes=["fb"])
     dma("s", "fd", T.fd[:, :], T.fb[:, 0:1], reads=["fb"], writes=["fd"])
     dma("s", "fo", T.fl[me], T.fb[:, 0:1], reads=["fb"], writes=["fl"], part=True)
-    send(near, 2, "af", lambda d: T.fb[:, 0:1], lambda d: T.fl[me], ["fb"])
+    dma("s", "w2", T.wt[:, 1024:2048], T.w[:, 1024:2048], writes=["wt"], part=True)
+    send(near, 3, "af", lambda d: T.fb[:, 0:1], lambda d: T.fl[me], ["fb"])
     for a in range(4):
         v("tr", T.fr[0:32, blk[a]], T.fb[blk[a], :], reads=["fb"], writes=["fr"], part=True)
     act(T.fr[blk[3], :], T.fr[0:32, :], F.Copy, reads=["fr"], writes=["frc"])
@@ -186,115 +226,86 @@ def rank_program(g, core, T, topo):
         v("scan", T.D1[:, half[k]], T.M1[:, half[u]], T.zb[:, 0:128], T.thk[:, h:h + 1], A.add, A.add,
           reads=["zb", "thk", "M1%d" % u], writes=["D1%d" % k])
     for h in range(2):
-        act(T.L1[:, half[h]], T.D1[:, half[0]], F.Sign, reads=["D10"], writes=["sa"], part=True,
-            bias=K * (16 * h - 0.5), accum_out=T.sa[:, h:h + 1])
-        v("scan", T.S1[:, half[h]], T.D1[:, half[1 + h]], T.tokv[:, 1:129], 0.0, A.max, A.min,
-          reads=["tokv", "D1%d" % (1 + h)], writes=["S1"], part=True)
-    for b in range(4):
-        act(T.lf1[0:32, 4 * b:4 * b + 2], T.sa[blk[b], 0:2], F.Identity, reads=["sa"], writes=["lf1"], part=True, bias=64.0, scale=0.5)
-        v("copy", T.lf1[0:32, 4 * b + 2:4 * b + 4], T.S1[blk[b], 127:256:128], reads=["S1"], writes=["lf1"], part=True)
+        act(T.L1[:, half[h]], T.D1[:, half[0]], F.Sign, reads=["D10"], writes=["Z1"], part=True,
+            bias=K * 16 * h, accum_out=T.Z1[:, 128 * h + 127:128 * h + 128])
+        v("scan", T.Z1[:, half[2 + h]], T.D1[:, half[1 + h]], T.two[:, :], -128.0, A.max, A.min,
+          reads=["two", "D1%d" % (1 + h)], writes=["Z1"], part=True)
+    for b in range(2):
+        act(T.lf1[0:32, 4 * b:4 * b + 4], T.Z1[blk[b], 127:512:128], F.Identity, reads=["Z1"], writes=["lf1"], part=True, bias=64.0, scale=0.5)
+        v("ts", T.lf1[0:32, 4 * b + 8:4 * b + 12], T.Z1[blk[b + 2], 127:512:128], 0.5, 64.0, A.mult, A.add, reads=["Z1"], writes=["lf1"], part=True)
     for b in range(4):
         v("copy", T.off1[blk[b], :], T.lf1[0:32, :], reads=["lf1"], writes=["off1"], part=True)
     O1 = ["off1", "xq"]
-    ms = slice(2 * me, 2 * me + 2)
-    v("copy", T.sq[:, :].bitcast(u32), T.xq[:, 0:130].bitcast(u32).indirect(T.off1[:, :]), reads=O1, writes=["sq"])
+    xq, xs = T.xq[:, 0:130].bitcast(u32), T.xs[:, 0:130]
+    for w in range(2):
+        v("copy", T.sq[:, cols[1][w]].bitcast(u32), xq.indirect(T.off1[:, offs[1][w]]), reads=O1, writes=["q1%d" % w])
     act(T.trow[:, :], T.tokv[:, 0:144].indirect(T.off1[:, :]), F.Copy, reads=O1 + ["tokv"], writes=["trow"])
-    act(T.ss[:, :], T.xs[:, 0:130].indirect(T.off1[:, :]), F.Copy, reads=O1, writes=["ss"])
-    v("copy", T.xh[:, blk[me]].bitcast(u32), T.xq[:, 0:130].bitcast(u32).indirect(T.off1[:, ms]), reads=O1, writes=["xh"], part=True)
-    v("copy", T.xhs[:, blk[me]], T.xs[:, 0:130].indirect(T.off1[:, ms]), reads=O1, writes=["xh"], part=True)
+    for w in range(2):
+        act(T.ss[:, cols[1][w]], xs.indirect(T.off1[:, offs[1][w]]), F.Copy, reads=O1, writes=["s1"], part=True)
+    v("copy", T.xh[:, blk[me]].bitcast(u32), xq.indirect(T.off1[:, 14:16]), reads=O1, writes=["xh"], part=True)
+    v("copy", T.xhs[:, blk[me]], xs.indirect(T.off1[:, 14:16]), reads=O1, writes=["xh"], part=True)
 
-    send(far, 2, "af", lambda d: T.fd[:, :], lambda d: T.fl[me], ["fd"])
-    send(others, 0, "a1", lambda d: T.sq[:, blk[d]].bitcast(u8), lambda d: T.xh[:, blk[me]].bitcast(u8), ["sq"])
-    send(others, 1, "a1", lambda d: T.ss[:, blk[d]], lambda d: T.xhs[:, blk[me]], ["ss"])
+    send(far, 3, "af", lambda d: T.fd[:, :], lambda d: T.fl[me], ["fd"])
+    columns(T.sq, T.ss, T.xh, T.xhs, lambda d: blk[me], CALLS1, ["q10", "q11", "s1", "s1"], ["a1"] * 4)
+    for o in range(2):
+        lands("x%d" % hs[o], "a1%d" % o)
     dma("s", "td", T.tokd[:, 0:CAPP, 0], T.trow[0:1, :], reads=["trow"], writes=["tokd"])
-    dma("s", "to", T.tokl[me:me + 1, 0:CAPP, 0], T.trow[0:1, blk[me]], reads=["trow"], writes=["tokl"], part=True)
-    lands("fl", "af", 2)
+    lands("fl", "af")
     dma("s", "fl", T.frl[0:8, :], T.fl[:, :, 0], reads=["fl"], writes=["frl"])
-    send(others, 0, "at", lambda d: T.tokd[d], lambda d: T.tokl[me], ["tokd"])
+    dma("s", "to", T.tokl[me:me + 1, 0:CAPP, 0], T.trow[0:1, blk[7]], reads=["trow"], writes=["tokl"], part=True)
+    send(others, 2, "at", lambda d: T.tokd[order.index(d)], lambda d: T.tokl[me], ["tokd"])
 
-    act(T.sgn[:, :], T.wt[:, 0:2 * SL], F.Identity, reads=["wt"], writes=["sgn1"], bias=1.0, scale=0.0)
     for t in range(4):
         act(T.r8t[:, t:512:4], T.zb[:, 0:128], F.Identity, reads=["r2t", "zb"], writes=["r8t"], part=True, bias=T.r2t[:, 28 + t:29 + t])
-    act(T.keep[:, :], T.zb[:, :], F.Identity, reads=["zb"], writes=["keep1"], bias=1.0)
-    act(T.pd[:, :], T.zb[:, :], F.Identity, reads=["zb"], writes=["pd1"], bias=BIG)
-    act(T.tokw[:, :], T.wt[:, 0:648], F.Identity, reads=["wt"], writes=["tokm"], bias=-1.0, scale=0.0)
-    v("qz", T.wq[:, :], T.ws[:, :], T.wt[:, :], reads=["wt"], writes=["wq"])
-    v("set", T.zt[:, :], 0.0, writes=["zt"])
+    const(T.keep[:, :], T.zb[:, :], "zb", 1, "keep1")
+    const(T.pd[:, :], T.zb[:, :], "zb", BIG, "pd1")
+    const(T.keep[:, 0:SL:CAPP], T.keep[:, 0:SL:CAPP], "keep1", 0, "keep")
+    const(T.tokw[:, :], T.tokv[:, :], "tokv", -1, "tokm")
+    OZ = ["offz", "xq"]
+    v("copy", T.xh[:, SL:SL + 32].bitcast(u32), xq.indirect(T.offz[:, :]), reads=OZ, writes=["xhz"], part=True)
+    v("copy", T.xhs[:, SL:SL + 32], xs.indirect(T.offz[:, :]), reads=OZ, writes=["xhz"], part=True)
     v("set", T.r2t[:, 4 * N:512], 0.0, writes=["r2z"])
-    v("set", T.ht[:, 1024:1032], 0.0, writes=["htz"])
-    v("set", T.offz[:, :], 0, writes=["offz"])
-    v("qz", T.xh[:, 256:384], T.xhs[:, 256:384], T.zt[:, :], reads=["zt"], writes=["xhz"])
-    v("qz", T.r2q[:, :], T.r2s[:, :], T.r2t[:, :], reads=["r2t", "r2z"], writes=["r2q"])
-    v("ts", T.p31[:, :], T.pp[:, :], 31, None, A.bitwise_and, reads=["pp"], writes=["p31"])
     v("set", T.ns[:, :], 0.0, writes=["ns"])
-    v("qz", T.r8q[:, :], T.r8s[:, :], T.r8t[:, :], reads=["r8t"], writes=["r8q"])
-    v("ts", T.ccol[:, :], T.p31[:, 0:1], BIG, None, A.mult, reads=["p31"], writes=["ccol"])
-    OZ = ["offz", "xhz"]
-    v("copy", T.l2q[:, blk[me]].bitcast(u32), T.xh[:, 256:384].bitcast(u32).indirect(T.offz[:, :]), reads=OZ, writes=["l2"], part=True)
-    v("copy", T.l2s[:, blk[me]], T.xhs[:, 256:384].indirect(T.offz[:, :]), reads=OZ, writes=["l2"], part=True)
-    v("ts", T.ig[:, :], T.cc[:, :], 32.0, float(CB), A.mult, A.add, reads=["cc"], writes=["ig"])
-    v("ts", T.mgt[:, :], T.ecol[:, :], float(me), -1.0, A.is_gt, A.mult, reads=["ecol"], writes=["mgt"])
-    v("tt", T.ih[:, :], T.ig[:, :], T.p15[:, :], A.add, reads=["ig", "p15"], writes=["ih"])
-    v("tt", T.mct[:, :], T.ecol[:, :], T.mgt[:, :], A.add, reads=["ecol", "mgt"], writes=["mct"])
-    v("copy", T.offh[:, :], T.ih[:, :], reads=["ih"], writes=["offh"])
-    v("ts", T.mcol[:, :], T.mct[:, :], 1.0, None, A.add, reads=["mct"], writes=["mcol"])
-    v("set", T.lim8[:, 0:7], 9e29, writes=["lim8"], part=True)
-    v("set", T.lim8[:, 7:8], -9e29, writes=["lim8"], part=True)
-    v("set", T.c128[:, :], 128.0, writes=["c128"])
-    v("set", T.keep[:, 0:SL:CAPP], 0.0, reads=["keep1"], writes=["keep"])
+    v("ts", T.mlt[:, :], T.ecol[:, :], float(me), None, A.is_lt, reads=["ecol"], writes=["mlt"])
+    v("qz", T.r2q[:, :], T.r2s[:, :], T.r2t[:, :], reads=["r2t", "r2z"], writes=["r2q"])
+    v("tt", T.mcol[:, :], T.ecol[:, :], T.mlt[:, :], A.add, reads=["ecol", "mlt"], writes=["mcol"])
+    v("set", T.ht[:, 1024:1032], 0.0, writes=["htz"])
     v("set", T.D2[:, :, SL:SL + 2], 0.0, writes=["D2z"])
-    v("set", T.hoc[:, 0:4:2], 0.0, writes=["hoc"], part=True)
-    v("set", T.hoc[:, 1:4:2], float(HO), writes=["hoc"], part=True)
-    for h in range(2):
-        k = slice(SL * h + 128 * h, SL * h + 128 * h + 128)
-        gp("sel", T.sgn[:, k], T.sgn[:, k], [[-1, 128]], A.not_equal, -1.0, 0, 1, reads=["sgn1"], writes=["sgn"], part=True)
-
-    v("ts", T.feq[0:8, :], T.frl[0:8, :], float(me), -BIG, A.is_equal, A.mult, reads=["frl"], writes=["feq"])
-    v("scan", T.ns[0:8, 0:128], T.feq[0:8, :], T.zb[0:8, 0:128], 0.5 * BIG, A.add, A.add, reads=["feq", "zb"], writes=["ns"])
-    v("tr", T.nt[:, :], T.ns[:, 127:159], reads=["ns"], writes=["nt"])
-    gp("all", T.pd[:, 0:SL:CAPP], T.nt[0:1, 0:N], 128, reads=["nt", "pd1"], writes=["pd"])
-
-    def pens(h):
-        v("scan", T.pen[:, half[h]], T.keep[:, half[h]], T.pd[:, half[h]], 0.0, A.mult, A.add, reads=["keep", "pd"], writes=["pen%d" % h])
-
-    def pcs(a):
-        act(T.Rm[blk[a], 0:18:9], T.pd[blk[a], 32 * a:SL:128], F.Identity, reads=["pd", "ccol"], writes=["Rmc"], part=True,
-            bias=T.ccol[blk[a], 0:1])
-    lands("tokl", "at", 0)
+    v("qz", T.r8q[:, :], T.r8s[:, :], T.r8t[:, :], reads=["r8t"], writes=["r8q"])
+    v("qz", T.wq[:, :], T.ws[:, :], T.wt[:, :], reads=["wt"], writes=["wq"])
+    lands("tokl", "at")
     dma("s", "tl", T.tokr[0:1, :], T.tokl[:, 0:CAPP, 0], reads=["tokl"], writes=["tokr"])
     dma("s", "vx", T.vxt[:, :], T.vx[:, :], writes=["vxt"])
     dma("s", "vh", T.vht[:, :], T.vh[:, :], writes=["vht"])
 
-    lands("xh", "a1", 0, 1)
     P = [[T.p1, T.p2, T.p3, T.p4], [T.p0, T.p5, T.p6, T.p7]]
     B = [["p1", "p2", "p3", "p4"], ["p0", "p5", "p6", "p7"]]
-    for h in range(2):
+    ROW, rw, PE, pe = [T.p1, T.p0], ["p1", "p0"], [T.p2, T.p5], ["p2", "p5"]
+
+    def made(h):
         for i in range(4):
             mm(P[h][i][:, 0:128], T.wq[:, half[i]], T.ws[:, half[i]], T.xh[:, half[h]], T.xhs[:, half[h]], True, True,
-               reads=["wq", "xh"], writes=[B[h][i]])
-    ROW, rw, PE, pe = [T.p1, T.p4], ["p1", "p4"], [T.p2, T.p3], ["p2", "p3"]
+               reads=["wq", "xh", "x%d" % h], writes=[B[h][i]])
+
+    def casts(h):
+        for i in range(4):
+            o = T.ht[:, 512 * h + i:512 * (h + 1):4]
+            if i == 3:
+                v("ts", o, P[h][i][:, 0:128], 0.0, 0.0625, A.max, A.mult, reads=[B[h][i]], writes=["ht%d" % h], part=True)
+            else:
+                act(o, P[h][i][:, 0:128], F.Relu, reads=[B[h][i]], writes=["ht%d" % h], part=True, scale=0.0625)
+
+    def pack(h):
+        k = slice(HO + 128 * h, XW if h else HO + 128)
+        v("qz", T.xh[:, k], T.xhs[:, k], T.ht[:, 512 * h:512 * (h + 1) + 8 * h], reads=["ht%d" % h, "htz"], writes=["h%d" % h])
 
     def products(h):
         k = slice(HO + 128 * h, HO + 128 * h + 128)
         mm(ROW[h][:, 0:128], T.r8q[:, :], T.r8s[:, :], T.xh[:, k], T.xhs[:, k], True, True, reads=["r8q", "h%d" % h], writes=[rw[h]])
         mm(PE[h][:, 0:128], T.xh[:, k], T.xhs[:, k], T.r2q[:, :], T.r2s[:, :], True, True, reads=["r2q", "h%d" % h], writes=[pe[h]])
 
-    def cast(q, h, i):
-        o = T.ht[:, 512 * h + i:512 * (h + 1):4]
-        if q == "v":
-            v("ts", o, P[h][i][:, 0:128], 0.0, 0.0625, A.max, A.mult, reads=[B[h][i]], writes=["ht%d" % h], part=True)
-        else:
-            act(o, P[h][i][:, 0:128], F.Relu, reads=[B[h][i]], writes=["ht%d" % h], part=True, scale=0.0625)
-    for h in range(2):
-        for i in range(4):
-            cast(("avav", "aaav")[h][i], h, i)
-        if h:
-            pens(0)
-        k = slice(HO + 128 * h, XW if h else HO + 128)
-        v("qz", T.xh[:, k], T.xhs[:, k], T.ht[:, 512 * h:512 * (h + 1) + 8 * h], reads=["ht%d" % h, "htz"], writes=["h%d" % h])
-        products(h)
-    for a in range(4):
-        pcs(a)
+    def pens(h):
+        v("scan", T.pen[:, half[h]], T.keep[:, half[h]], T.pd[:, half[h]], 0.0, A.mult, A.add, reads=["keep", "pd"], writes=["pen%d" % h])
 
     def second(h):
         k = 9 * h
@@ -302,91 +313,113 @@ def rank_program(g, core, T, topo):
 
     def away(h):
         v("tt", T.E1[:, half[h]], ROW[h][:, 0:128], T.pen[:, half[h]], A.max, reads=[rw[h], "pen%d" % h], writes=["E1"], part=True)
-    pens(1)
-    away(0)
-    second(0)
-    away(1)
-    second(1)
 
     def number(h):
         k = 9 * h
         act(T.mj[:, 8 * h:8 * h + 8], T.Rm[:, k:k + 8], F.Sign, reads=["Rm%d" % h, "Rmc"], writes=["mm%d" % h],
             bias=T.Rm[:, k + 7:k + 8], scale=-1.0, accum_out=T.mm[:, h:h + 1])
         act(T.mp[:, h:h + 1], T.mm[:, h:h + 1], F.Copy, reads=["mm%d" % h], writes=["mp%d" % h])
-    number(0)
-    for h in range(2):
+    v("ts", T.feq[0:8, :], T.frl[0:8, :], float(me), -BIG, A.is_equal, A.mult, reads=["frl"], writes=["feq"])
+    v("scan", T.ns[0:8, 0:128], T.feq[0:8, :], T.zb[0:8, 0:128], 0.5 * BIG, A.add, A.add, reads=["feq", "zb"], writes=["ns"])
+    v("tr", T.nt[:, :], T.ns[:, 127:159], reads=["ns"], writes=["nt"])
+    gp("all", T.pd[:, 0:SL:CAPP], T.nt[0:1, 0:N], 128, reads=["nt", "pd1"], writes=["pd"])
+    made(hs[0])
+    made(hs[1])
+    casts(hs[0])
+    pack(hs[0])
+    products(hs[0])
+    casts(hs[1])
+    pens(hs[0])
+    for a in range(4):
+        act(T.Rm[blk[a], 0:18:9], T.pd[blk[a], 32 * a:SL:128], F.Identity, reads=["pd", "ccol"], writes=["Rmc"], part=True,
+            bias=T.ccol[blk[a], 0:1])
+    pack(hs[1])
+    products(hs[1])
+    second(hs[0])
+    pens(hs[1])
+    away(hs[0])
+    number(hs[0])
+    away(hs[1])
+    second(hs[1])
+    for h in hs:
         e8 = T.Rm[:, 9 * h + 8:9 * h + 9]
         act(T.SJ[:, row[h]], T.E1[:, :], F.Sign, reads=["E1", "Rm%d" % h], writes=["sg%d" % h],
             bias=e8, scale=-1.0, accum_out=T.sg[:, h:h + 1])
         v("ts", T.EQ[:, row[h]], T.E1[:, :], e8, None, A.is_equal, reads=["E1", "Rm%d" % h], writes=["EQ%d" % h])
-    number(1)
+    number(hs[1])
 
-    def rank(h):
-        v("scan", T.FS[:, row[h]], T.sgn[:, row[h]], T.EQ[:, row[h]], T.sg[:, h:h + 1], A.mult, A.add,
-          reads=["sgn", "EQ%d" % h, "sg%d" % h], writes=["FS%d" % h])
-    rank(0)
-    rank(1)
-    for h in range(2):
+    for h in hs:
+        v("scan", T.FS[:, row[h]], T.sgn[:, 128 - 128 * h:384 - 128 * h], T.EQ[:, row[h]], T.sg[:, h:h + 1], A.mult, A.add,
+          reads=["sgn", "sgn1", "EQ%d" % h, "sg%d" % h], writes=["FS%d" % h])
+    for h in hs:
         v("ts", T.fb2[:, blk[h]], T.c128[:, :], T.FS[:, SL * h + SL - 1:SL * h + SL], T.mp[:, h:h + 1], A.is_lt, A.mult,
           reads=["c128", "FS%d" % h, "mp%d" % h], writes=["fb2"], part=True)
+    part = [slice(0, 64), slice(64, 128)]
     for a in range(4):
-        v("tr", T.fr2[0:32, a, :], T.fb2[blk[a], :], reads=["fb2"], writes=["fr2"], part=True)
-    act(T.fr2[blk[3], :, :], T.fr2[0:32, :, :], F.Copy, reads=["fr2"], writes=["fr2c"])
-    for b in range(1, 3):
-        v("copy", T.fr2[blk[b], :, :], T.fr2[0:32, :, :], reads=["fr2"], writes=["fr2a"], part=b > 1)
-    for u in range(2):
-        for h in range(2):
-            v("ts", T.M2[:, half[2 * u + h]], T.fr2[:, :, blk[h]], T.mcol[:, u:u + 1], -K, A.is_equal, A.mult,
-              reads=["fr2", "fr2a", "fr2c", "mcol"], writes=["M2%d" % u], part=True)
+        v("tr", T.fr2[0:32, :, blk[a]], T.fb2[blk[a], :], reads=["fb2"], writes=["fr2%d" % (a // 2)], part=True)
+    for k in range(2):
+        act(T.fr2[blk[3], :, part[k]], T.fr2[0:32, :, part[k]], F.Copy, reads=["fr2%d" % k], writes=["fr2c%d" % k])
+        for b in range(1, 3):
+            v("copy", T.fr2[blk[b], :, part[k]], T.fr2[0:32, :, part[k]], reads=["fr2%d" % k], writes=["fr2a%d" % k], part=True)
+    for k in range(2):
+        for u in range(2):
+            v("ts", T.M2[:, 2 * u:2 * u + 2, part[k]], T.fr2[:, :, part[k]], T.mcol[:, u:u + 1], -K, A.is_equal, A.mult,
+              reads=["fr2%d" % k, "fr2a%d" % k, "fr2c%d" % k, "mcol"], writes=["M2%d" % u], part=True)
     for s in range(N):
         act(T.tokw[0:1, blk[s]], T.tokr[0:1, blk[s]], F.Identity, reads=["tokr", "tokm"], writes=["tokw"], part=True, bias=float(TK * s))
-    for u in range(2):
-        v("scan", T.D2[:, u, 0:SL], T.M2[:, row[u]], T.zb[:, :], T.thk[:, 0:1], A.add, A.add, reads=["zb", "thk", "M2%d" % u], writes=["D2%d" % u])
+    for h in range(2):
+        for u in range(2):
+            v("scan", T.D2[:, u, half[h]], T.M2[:, 2 * u + h, :], T.zb[:, 0:128], T.D2[:, u, 127:128] if h else T.thk[:, 2:3], A.add, A.add,
+              reads=["zb", "thk", "M2%d" % u] + ["D2%d" % u] * h, writes=["D2%d" % u], part=True)
     for u in range(2):
         v("scan", T.S2[:, u, 0:SL + 1], T.D2[:, u, 0:SL + 1], T.tokv[:, 1:SL + 2], 0.0, A.max, A.min,
-          reads=["tokv", "D2z", "D2%d" % u], writes=["S2"], part=True)
-    for b in range(3):
-        v("tt", T.lf2[0:32, 4 * b:4 * b + 4], T.S2[blk[b], :, SL - 1:SL + 1], T.hoc[blk[b], :], A.add, reads=["S2", "hoc"], writes=["lf2"], part=True)
-    for u in range(2):
-        act(T.lf2[0:32, 12 + 2 * u:14 + 2 * u], T.hoc[blk[3], 0:2], F.Identity, reads=["S2", "hoc"], writes=["lf2"], part=True,
-            bias=T.S2[blk[3], u, SL:SL + 1])
+          reads=["tokv", "D2z", "D2%d" % u], writes=["S2%d" % u])
+    for b, u in [(2, 0), (3, 0), (2, 1)]:
+        act(T.lf2[0:32, 4 * b + 2 * u:4 * b + 2 * u + 2], T.hoc[blk[b], 0:2], F.Identity, reads=["S2%d" % u, "hoc"], writes=["lf2"], part=True,
+            bias=T.S2[blk[b], u, SL:SL + 1])
+    for b in range(2):
+        v("tt", T.lf2[0:32, 4 * b:4 * b + 4], T.S2[blk[b], :, SL - 1:SL + 1], T.hoc[blk[b], :], A.add, reads=["S20", "S21", "hoc"], writes=["lf2"], part=True)
+    v("copy", T.offw[0:32, 0:7], T.lf2[0:32, 0:14:2], reads=["lf2"], writes=["offw"])
+    act(T.wr[:, :], T.tokw[:, :].indirect(T.offw[:, :]), F.Copy, reads=["offw", "tokw", "tokm"], writes=["wr"])
     for b in range(4):
-        v("copy", T.off2[blk[b], :], T.lf2[0:32, :], reads=["lf2"], writes=["off2"], part=True)
-    O2 = ["off2"]
-    XR = O2 + ["xh", "xhz", "h0", "h1"]
-    v("copy", T.s2q[:, :].bitcast(u32), T.xh[:, 0:XW].bitcast(u32).indirect(T.off2[:, :]), reads=XR, writes=["s2q"])
-    act(T.wr[:, :], T.tokw[:, 0:XW].indirect(T.off2[:, :]), F.Copy, reads=O2 + ["tokw", "tokm"], writes=["wr"])
-    act(T.s2s[:, :], T.xhs[:, 0:XW].indirect(T.off2[:, :]), F.Copy, reads=XR, writes=["s2s"])
-    send(others, 0, "a2", lambda d: T.s2q[:, blk[d]].bitcast(u8), lambda d: T.l2q[:, blk[me]].bitcast(u8), ["s2q"])
-    send(others, 1, "a2", lambda d: T.s2s[:, blk[d]], lambda d: T.l2s[:, blk[me]], ["s2s"])
+        v("copy", T.off2[blk[b], :], T.lf2[0:32, 0:14], reads=["lf2"], writes=["off2"], part=True)
+    XR = ["off2", "xh", "x0", "x1", "xhz", "h0", "h1"]
+    for w in range(2):
+        v("copy", T.s2q[:, cols[2][w]].bitcast(u32), T.xh[:, 0:XW].bitcast(u32).indirect(T.off2[:, offs[2][w]]), reads=XR, writes=["q2%d" % w])
+        act(T.s2s[:, cols[2][w]], T.xhs[:, 0:XW].indirect(T.off2[:, offs[2][w]]), F.Copy, reads=XR, writes=["s2%d" % w])
+    columns(T.s2q, T.s2s, T.l2q, T.l2s, lambda d: blk[come[d].index(me)], CALLS2, ["q20", "s20", "s21", "q21"], ["a20", "a20", "a2s", "a21"])
+    for k in "0s1":
+        lands("l2" + k, "a2" + k)
 
-    dma("s", "wd", T.whod[:, 0:2 * CB, 0], T.wr[0:1, :], reads=["wr"], writes=["whod"])
-    send(others, 0, "aw", lambda d: T.whod[d], lambda d: T.whol[me], ["whod"])
+    dma("s", "wd", T.whod[:, 0:CB, 0], T.wr[0:1, :], reads=["wr"], writes=["whod"])
+    send(others, 2, "aw", lambda d: T.whod[order.index(d)], lambda d: T.whol[me], ["whod"])
+    for a in range(N):
+        v("ts", T.offh[:, a:a + 1], T.p15[:, 0:1], float(32 * come[me].index(a) + CB), None, A.add, reads=["p15"], writes=["offh"], part=True)
+    v("copy", T.l2q[:, blk[n1]].bitcast(u32), xq.indirect(T.offz[:, :]), reads=OZ, writes=["l2z"], part=True)
+    act(T.l2s[:, blk[n1]], xs.indirect(T.offz[:, :]), F.Copy, reads=OZ, writes=["l2z"], part=True)
     v("qz", T.vxq[:, :], T.vxs[:, :], T.vxt[:, :], reads=["vxt"], writes=["vxq"])
     v("qz", T.vhq[:, :], T.vhs[:, :], T.vht[:, :], reads=["vht"], writes=["vhq"])
+    const(T.ysb[:, CB * me:CB * me + CB], T.zb[:, 0:CB], "zb", 0, "ysb", True)
 
-    lands("l2", "a2", 0, 1)
+    act(T.hs[:, :], T.l2s[:, :].indirect(T.offh[:, :]), F.Copy, reads=["l2z", "l20", "l2s", "offh"], writes=["hs"])
+    for k in range(4):
+        dma("sa"[k % 2], "o%d" % k, T.osc[4 * k:4 * k + 4, :], T.hs[32 * k:32 * k + 4, :], reads=["hs"], writes=["osc%d" % k])
     Y, yt = [T.p0, T.p5], ["p0", "p5"]
     for q in range(2):
-        n, t = (144, 128)[q], yt[q]
+        n, t, got = (144, 128)[q], yt[q], ["l2z", "l20"] + ["l2s", "l21"] * q
         k, j = slice(112 * q, 112 * q + n), slice(112 * q + CB, 112 * q + CB + n)
-        mm(Y[q][:, 0:n], T.vxq[:, :], T.vxs[:, :], T.l2q[:, k], T.l2s[:, k], True, False, reads=["vxq", "l2"], writes=[t])
-        mm(Y[q][:, 0:n], T.vhq[:, :], T.vhs[:, :], T.l2q[:, j], T.l2s[:, j], False, True, reads=["vhq", "l2"], writes=[t], part=True)
-    v("copy", T.hq[:, :].bitcast(u32), T.l2q[:, :].bitcast(u32).indirect(T.offh[:, :]), reads=["l2", "offh"], writes=["hq"])
-    act(T.hs[:, :], T.l2s[:, :].indirect(T.offh[:, :]), F.Copy, reads=["l2", "offh"], writes=["hs"])
-    for a in range(N):
-        k = 32 * a - 112 * (a // 5)
-        o, i = T.ysb[:, CB * a:CB * a + CB], Y[a // 5][:, k:k + CB]
-        if a < 5:
-            v("copy", o, i, reads=[yt[0]], writes=["ysb"], part=True)
+        mm(Y[q][:, 0:n], T.vxq[:, :], T.vxs[:, :], T.l2q[:, k], T.l2s[:, k], True, False, reads=["vxq"] + got, writes=[t])
+        mm(Y[q][:, 0:n], T.vhq[:, :], T.vhs[:, :], T.l2q[:, j], T.l2s[:, j], False, True, reads=["vhq"] + got, writes=[t], part=True)
+    for c in range(N):
+        a, k = come[me][c], 32 * c - 112 * (c > n1)
+        if c == n1:
+            v("copy", T.hq[:, :].bitcast(u32), T.l2q[:, :].bitcast(u32).indirect(T.offh[:, :]), reads=["l2z", "l20", "l21", "offh"], writes=["hq"])
         else:
-            act(o, i, F.Copy, reads=[yt[1]], writes=["ysb"], part=True)
-    dma("s", "oc", T.oc[:, :], T.hq[:, :].bitcast(u8), reads=["hq"], writes=["oc"])
-    for k in range(4):
-        dma("s" if k < 2 else "a", "o%d" % k, T.osc[4 * k:4 * k + 4, :], T.hs[32 * k:32 * k + 4, :], reads=["hs"], writes=["osc%d" % k])
+            v("copy", T.ysb[:, CB * a:CB * a + CB], Y[c > n1][:, k:k + CB], reads=[yt[c > n1]], writes=["ysb"], part=True)
+    dma("a", "oc", T.oc[:, :], T.hq[:, :].bitcast(u8), reads=["hq"], writes=["oc"])
     dma("s", "y", T.y[:, :], T.ysb[:, :], reads=["ysb"], writes=["y"])
-    lands("whol", "aw", 0)
-    dma("s", "who", T.who[0:1, :], T.whol[:, 0:CB, 0], reads=["whol"], writes=["who"])
+    lands("whol", "aw")
+    dma("a", "who", T.who[0:1, :], T.whol[:, 0:CB, 0], reads=["whol"], writes=["who"])
     for sem in sorted(cnt):
         if max(seen[q].get(sem, 0) for q in eng) < cnt[sem]:
-            need("a" if sem in ("d_o2", "d_o3") else "s" if sem[:2] == "d_" else "g", [(sem, cnt[sem])])
+            need(queue.get(sem, "g"), [(sem, cnt[sem])])

from concourse.bass import DstId, RemoteDMATransfer
from concourse.mybir import dt, AluOpType as A, ActivationFunctionType as F

N = 8
TK = 128
CAPP = 32
CB = 16
SL = N * CAPP
OUT = SL - CAPP
HO = 384
XW = 642
BIG = 2.0 ** 96
K = 256.0
CALLS1 = "q4 q5 s6 s7"
CALLS2 = "q0 s0 s1 q1"

SCRATCH = {}


def _declare(kind, dtype, **bufs):
    for name, n in bufs.items():
        SCRATCH[name] = (kind, n if isinstance(n, list) else [128, n], dtype)


_declare("sbuf", "bfloat16", xt=520, rtt=512, wt=2048, r2t=512, r8t=512, vxt=512, vht=512, ht=1032)
_declare("sbuf", "float8_e4m3fn_x4", xq=136, rq=128, wq=512, r2q=128, r8q=128, vxq=128, vhq=128, sq=OUT, xh=648, s2q=OUT, l2q=SL, hq=128)
_declare("sbuf", "uint8", xs=136, rs=128, ws=512, r2s=128, r8s=128, vxs=128, vhs=128, ss=OUT, xhs=648, s2s=OUT, l2s=SL, hs=128)
_declare("dram", "bfloat16", fd=[128, 1], fl=[N, 128, 1], tokd=[N, 128, 1], tokl=[N, 128, 1])
_declare("dram", "float32", whod=[N, 128, 1], whol=[N, 128, 1])
_declare("sbuf", "int32", pp=8, p15=8, p31=8)
_declare("sbuf", "float32", thk=3, ccol=1, ecol=2, mlt=2, mcol=2, neg8=8, lim8=8, hoc=4, m1=128)
_declare("sbuf", "bfloat16", zb=SL, c128=32, keep=SL, sgn=384, tokv=SL + 2, two=128)
_declare("sbuf", "uint16", offz=2, offh=8, offw=8, off1=16, off2=14)
_declare("sbuf", "float32", R=8, first=1, Z1=512, lf1=[32, 16], lf2=[32, 16], E1=SL, Rm=18, mj=16, mm=2, sg=2, tokw=SL + 2, wr=128, ysb=128)
_declare("sbuf", "bfloat16", fb=32, fr=128, M1=256, D1=384, L1=256, trow=SL, tokr=SL, frl=[32, 128], feq=[32, 128],
         ns=[32, 160], nt=[32, 32], pd=SL, pen=SL, EQ=2 * SL, FS=2 * SL, SJ=2 * SL, mp=2, fb2=64, fr2=[128, 2, 128],
         M2=[128, 4, 128], D2=[128, 2, SL + 2], S2=[128, 2, SL + 2])
_declare("psum", "float32", p0=512, p1=512, p2=512, p3=512, p4=512, p5=512, p6=512, p7=512)
_DMAS = ["x", "rt", "w", "w2", "r2a", "r2b", "vx", "vh", "fd", "fo", "fl", "td", "to", "tl", "wd", "wo", "ti", "wi",
         "y", "oc", "o0", "o1", "o2", "o3", "who"]
SEMAPHORES = ["qv", "qa", "qt", "qg", "af", "a10", "a11", "at", "a20", "a21", "a2s", "aw", "loc"] + ["d_" + k for k in _DMAS]


def plan(T, topo, s):
    c = T.cores[s]
    near = [r for r in range(N) if r != s and topo.chip(T.cores[r]) == topo.chip(c)]

    def hops(r):
        a, b = topo.chip(c), topo.chip(T.cores[r])
        return 0 if topo.mates(a, b) else 1 if topo.same_plane(a, b) else 2
    far = sorted([r for r in range(N) if r != s and r not in near], key=lambda r: (hops(r), topo.die(T.cores[r]) == topo.die(c)))
    e = topo.engines(c, T.cores[far[0]])
    k = [x for x in topo.engines(c, T.cores[near[0]]) if x not in e][0:4:2]
    four = {far[0]: e[0:2], far[2]: e[2:4], far[4]: e[4:6], far[5]: e[6:8]}
    two = {far[1]: e[0:4], far[3]: e[4:8]}
    short = {**{d: [x] for d, x in zip(far, e)}, near[0]: k[:1]}
    firsts = {**{d: [e[1 + 4 * (i % 2)]] for i, d in enumerate(far)}, near[0]: e}
    switch = {far[2]: e[0:2], far[4]: e[2:4], far[3]: e[4:6], far[5]: e[6:8], near[0]: k}
    mates = {far[0]: e[0:4], far[1]: e[4:8]}
    return {**four, near[0]: k}, two, short, firsts, four, {near[0]: k, **two}, switch, mates


def rank_program(g, core, T, topo):
    me = T.rank_of(core)
    if me is None:
        return
    S = T.sem
    plans = [plan(T, topo, s) for s in range(N)]
    others = [r for r in range(N) if r != me]
    far = [r for r in others if topo.chip(T.cores[r]) != topo.chip(core)]
    near = [r for r in others if r not in far]
    order = list(plans[me][0]) + list(plans[me][1]) + [me]
    n1 = len(plans[me][0])
    hs = [1 - me // 4, me // 4]
    come = [[s for s in range(N) if d in plans[s][0]] + [d] + [s for s in range(N) if d in plans[s][1]] for d in range(N)]
    eng = {"v": g.vector, "a": g.scalar, "t": g.tensor, "s": g.sync, "g": g}
    vec = g.vector
    V = {"set": vec.memset, "copy": vec.tensor_copy, "ts": vec.tensor_scalar, "tt": vec.tensor_tensor,
         "scan": vec.tensor_tensor_scan, "tr": vec.transpose, "qz": vec.quantize_mx}
    G = {"iota": g.iota, "sel": g.affine_select, "all": g.partition_broadcast}
    cnt, queue = {}, {}
    seen = {q: {} for q in eng}
    wr, rd = {}, {}

    def need(q, evs):
        m = {}
        for sem, n in evs:
            m[sem] = max(n, m.get(sem, 0))
        for sem in sorted(m):
            if seen[q].get(sem, 0) < m[sem]:
                eng[q].wait_ge(S[sem], m[sem])
                seen[q][sem] = m[sem]

    def before(q, reads, writes, part):
        evs = [e for t in reads for e in wr[t]]
        if not part:
            evs += [e for t in writes for e in wr.get(t, []) + rd.get(t, [])]
        need(q, evs)

    def after(ev, reads, writes, part):
        for t in reads:
            rd.setdefault(t, []).append(ev)
        for t in writes:
            wr[t] = (wr.get(t, []) if part else []) + [ev]
            if not part:
                rd[t] = []

    def op(q, f, args, reads=(), writes=(), part=False, **kw):
        before(q, reads, writes, part)
        sem = "q" + q
        cnt[sem] = cnt.get(sem, 0) + 1
        f(*args, **kw).then_inc(S[sem], 1)
        after((sem, cnt[sem]), reads, writes, part)

    def v(name, *args, **kw):
        op("v", V[name], args, **kw)

    def act(*args, **kw):
        op("a", g.scalar.activation, args, **kw)

    def const(out, src, tag, c, name, part=False):
        act(out, src, F.Identity, reads=[tag], writes=[name], part=part, bias=float(c), scale=0.0)

    def mm(*args, **kw):
        op("t", g.tensor.matmul_mx, args, **kw)

    def gp(name, *args, **kw):
        op("g", G[name], args, **kw)

    def dma(q, key, out, in_, reads=(), writes=(), part=False):
        before(q, reads, writes, part)
        eng[q].dma_start(out, in_).then_inc(S["d_" + key], 16)
        cnt["d_" + key], queue["d_" + key] = 16, q
        after(("d_" + key, 16), reads, writes, part)

    def send(to, which, sem, src, dst, reads):
        def name(r):
            return sem + str(hs.index(r // 4)) if sem == "a1" else sem
        need("g", [e for t in reads for e in wr[t]])
        tr = []
        for es in sorted({tuple(plans[me][which][d]) for d in to}):
            ds = [d for d in to if tuple(plans[me][which][d]) == es]
            ad = [topo.addr(T.cores[d]) for d in ds]
            tr.append(RemoteDMATransfer(dst_ids=[DstId(rid=a[0], pnc=a[1]) for a in ad], dma_engine_mask=sum(1 << e for e in es),
                                        remote_sem=S[name(ds[0])], srcs=[src(ds[0])], dsts=[dst(d) for d in ds]))
            cnt["loc"] = cnt.get("loc", 0) + len(es)
        g.remote_dma_fused(tr, local_sem=S["loc"])
        for s in to:
            cnt[name(s)] = cnt.get(name(s), 0) + len(plans[s][which][me])

    def lands(tag, sem):
        wr.setdefault(tag, []).append((sem, cnt[sem]))

    u8, u32 = dt.uint8, dt.uint32
    blk = [slice(32 * b, 32 * b + 32) for b in range(N)]
    half = [slice(128 * h, 128 * h + 128) for h in range(4)]
    row = [slice(SL * h, SL * h + SL) for h in range(2)]
    cols = {st: [slice(0, 32 * n), slice(32 * n, OUT)] for st, n in ((1, n1 - 1), (2, n1))}
    offs = {st: [slice(0, 2 * n), slice(2 * n, 14)] for st, n in ((1, n1 - 1), (2, n1))}

    def columns(q, s, lq, ls, at, calls, tags, sems):
        for (kind, w), tag, sem in zip(calls.split(), tags, sems):
            w = int(w)
            if kind == "q":
                send(list(plans[me][w]), w, sem, lambda d: q[:, blk[order.index(d)]].bitcast(u8), lambda d: lq[:, at(d)].bitcast(u8), [tag])
            else:
                send(list(plans[me][w]), w, sem, lambda d: s[:, blk[order.index(d)]], lambda d: ls[:, at(d)], [tag])

    dma("s", "x", T.xt[:, 0:512], T.x[:, :], writes=["xt"], part=True)
    dma("a", "rt", T.rtt[:, 0:4 * N], T.rt[:, 0:4 * N], writes=["rtt"], part=True)
    dma("s", "w", T.wt[:, 0:1024], T.w[:, 0:1024], writes=["wt"], part=True)
    if me > 0:
        dma("s", "r2a", T.r2t[:, 0:4 * me], T.r2[:, 0:4 * me], writes=["r2t"], part=True)
    dma("s", "r2b", T.r2t[:, 4 * me:4 * N], T.r2[:, 4 * me + 4:4 * N + 4], writes=["r2t"], part=True)

    fl = {"allow_small_or_imprecise_dtypes": True}
    gp("iota", T.pp[:, :], [[0, 8]], 0, 1, writes=["pp"])
    gp("iota", T.tokv[:, :], [[1, SL + 2]], 0, 0, writes=["tokv"], **fl)
    v("set", T.zb[:, :], 0.0, writes=["zb"])
    v("set", T.rtt[:, 4 * N:512], 0.0, writes=["rtt"], part=True)
    v("set", T.xt[:, 512:520], 0.0, writes=["xt"], part=True)
    v("set", T.neg8[:, :], -9e29, writes=["neg8"])
    v("ts", T.p15[:, :], T.pp[:, :], 15, None, A.bitwise_and, reads=["pp"], writes=["p15"])
    v("ts", T.p31[:, :], T.pp[:, :], 31, None, A.bitwise_and, reads=["pp"], writes=["p31"])
    v("set", T.offz[:, :], TK, writes=["offz"])
    for u in range(3):
        v("ts", T.thk[:, u:u + 1], T.p15[:, 0:1], (0.5, 16.5, 1.0)[u], K, A.add, A.mult, reads=["p15"], writes=["thk"], part=True)
    v("ts", T.ccol[:, :], T.p31[:, 0:1], BIG, None, A.mult, reads=["p31"], writes=["ccol"])
    v("set", T.offw[:, :], 0, writes=["offw"])
    const(T.m1[:, :], T.zb[:, 0:128], "zb", -1, "m1")
    const(T.sgn[:, 0:SL], T.zb[:, :], "zb", 1, "sgn1", True)
    const(T.sgn[:, SL:384], T.zb[:, 0:128], "zb", 1, "sgn1", True)
    gp("sel", T.sgn[:, half[1]], T.sgn[:, half[1]], [[-1, 128]], A.not_equal, -1.0, 0, 1, reads=["sgn1"], writes=["sgn"])
    dma("s", "ti", T.tokd[:, :, 0], T.zb[0:N, 0:128], reads=["zb"], writes=["tokd"])
    dma("s", "wo", T.whol[me:me + 1, 0:CB, 0], T.m1[0:1, 0:CB], reads=["m1"], writes=["whol"], part=True)
    dma("s", "wi", T.whod[:, :, 0], T.m1[0:N, :], reads=["m1"], writes=["whod"])
    act(T.two[:, :], T.tokv[:, 1:129], F.Identity, reads=["tokv"], writes=["two"], bias=-128.0, scale=2.0)
    for b in range(4):
        e0, e1 = order[2 * b], order[2 * b + 1]
        act(T.ecol[blk[b], :], T.tokv[blk[b], 0:2], F.Identity, reads=["tokv"], writes=["ecol"], part=True, bias=float(e0), scale=float(e1 - e0))
    const(T.lim8[:, 0:7], T.zb[:, 0:7], "zb", 9e29, "lim8", True)
    const(T.lim8[:, 7:8], T.zb[:, 0:1], "zb", -9e29, "lim8", True)
    const(T.c128[:, :], T.zb[:, 0:32], "zb", 128, "c128")
    const(T.hoc[:, 0:4:2], T.zb[:, 0:2], "zb", 0, "hoc", True)
    const(T.hoc[:, 1:4:2], T.zb[:, 0:2], "zb", HO, "hoc", True)

    v("qz", T.rq[:, :], T.rs[:, :], T.rtt[:, :], reads=["rtt"], writes=["rq"])
    v("qz", T.xq[:, 0:130], T.xs[:, 0:130], T.xt[:, :], reads=["xt"], writes=["xq"])
    mm(T.p0[:, 0:128], T.xq[:, 0:128], T.xs[:, 0:128], T.rq[:, :], T.rs[:, :], True, True, reads=["xq", "rq"], writes=["p0"])
    v("scan", T.R[:, :], T.p0[:, 0:8], T.neg8[:, :], -9e29, A.max, A.max, reads=["p0", "neg8"], writes=["R"])
    act(T.mj[:, 0:8], T.R[:, :], F.Sign, reads=["R"], writes=["first"], bias=T.R[:, 7:8], scale=-1.0, accum_out=T.first[:, 0:1])
    v("ts", T.fb[:, :], T.zb[:, 0:32], T.first[:, 0:1], None, A.add, reads=["zb", "first"], writes=["fb"])
    dma("s", "fd", T.fd[:, :], T.fb[:, 0:1], reads=["fb"], writes=["fd"])
    dma("s", "fo", T.fl[me], T.fb[:, 0:1], reads=["fb"], writes=["fl"], part=True)
    dma("s", "w2", T.wt[:, 1024:2048], T.w[:, 1024:2048], writes=["wt"], part=True)
    send(near, 3, "af", lambda d: T.fb[:, 0:1], lambda d: T.fl[me], ["fb"])
    for a in range(4):
        v("tr", T.fr[0:32, blk[a]], T.fb[blk[a], :], reads=["fb"], writes=["fr"], part=True)
    act(T.fr[blk[3], :], T.fr[0:32, :], F.Copy, reads=["fr"], writes=["frc"])
    for b in range(1, 3):
        v("copy", T.fr[blk[b], :], T.fr[0:32, :], reads=["fr"], writes=["fra"], part=b > 1)
    for u in range(2):
        v("ts", T.M1[:, half[u]], T.fr[:, :], T.ecol[:, u:u + 1], -K, A.is_equal, A.mult,
          reads=["fr", "fra", "frc", "ecol"], writes=["M1%d" % u])
    for k, (u, h) in enumerate([(0, 0), (1, 0), (1, 1)]):
        v("scan", T.D1[:, half[k]], T.M1[:, half[u]], T.zb[:, 0:128], T.thk[:, h:h + 1], A.add, A.add,
          reads=["zb", "thk", "M1%d" % u], writes=["D1%d" % k])
    for h in range(2):
        act(T.L1[:, half[h]], T.D1[:, half[0]], F.Sign, reads=["D10"], writes=["Z1"], part=True,
            bias=K * 16 * h, accum_out=T.Z1[:, 128 * h + 127:128 * h + 128])
        v("scan", T.Z1[:, half[2 + h]], T.D1[:, half[1 + h]], T.two[:, :], -128.0, A.max, A.min,
          reads=["two", "D1%d" % (1 + h)], writes=["Z1"], part=True)
    for b in range(2):
        act(T.lf1[0:32, 4 * b:4 * b + 4], T.Z1[blk[b], 127:512:128], F.Identity, reads=["Z1"], writes=["lf1"], part=True, bias=64.0, scale=0.5)
        v("ts", T.lf1[0:32, 4 * b + 8:4 * b + 12], T.Z1[blk[b + 2], 127:512:128], 0.5, 64.0, A.mult, A.add, reads=["Z1"], writes=["lf1"], part=True)
    for b in range(4):
        v("copy", T.off1[blk[b], :], T.lf1[0:32, :], reads=["lf1"], writes=["off1"], part=True)
    O1 = ["off1", "xq"]
    xq, xs = T.xq[:, 0:130].bitcast(u32), T.xs[:, 0:130]
    for w in range(2):
        v("copy", T.sq[:, cols[1][w]].bitcast(u32), xq.indirect(T.off1[:, offs[1][w]]), reads=O1, writes=["q1%d" % w])
    act(T.trow[:, :], T.tokv[:, 0:144].indirect(T.off1[:, :]), F.Copy, reads=O1 + ["tokv"], writes=["trow"])
    for w in range(2):
        act(T.ss[:, cols[1][w]], xs.indirect(T.off1[:, offs[1][w]]), F.Copy, reads=O1, writes=["s1"], part=True)
    v("copy", T.xh[:, blk[me]].bitcast(u32), xq.indirect(T.off1[:, 14:16]), reads=O1, writes=["xh"], part=True)
    v("copy", T.xhs[:, blk[me]], xs.indirect(T.off1[:, 14:16]), reads=O1, writes=["xh"], part=True)

    send(far, 3, "af", lambda d: T.fd[:, :], lambda d: T.fl[me], ["fd"])
    columns(T.sq, T.ss, T.xh, T.xhs, lambda d: blk[me], CALLS1, ["q10", "q11", "s1", "s1"], ["a1"] * 4)
    for o in range(2):
        lands("x%d" % hs[o], "a1%d" % o)
    dma("s", "td", T.tokd[:, 0:CAPP, 0], T.trow[0:1, :], reads=["trow"], writes=["tokd"])
    lands("fl", "af")
    dma("s", "fl", T.frl[0:8, :], T.fl[:, :, 0], reads=["fl"], writes=["frl"])
    dma("s", "to", T.tokl[me:me + 1, 0:CAPP, 0], T.trow[0:1, blk[7]], reads=["trow"], writes=["tokl"], part=True)
    send(others, 2, "at", lambda d: T.tokd[order.index(d)], lambda d: T.tokl[me], ["tokd"])

    for t in range(4):
        act(T.r8t[:, t:512:4], T.zb[:, 0:128], F.Identity, reads=["r2t", "zb"], writes=["r8t"], part=True, bias=T.r2t[:, 28 + t:29 + t])
    const(T.keep[:, :], T.zb[:, :], "zb", 1, "keep1")
    const(T.pd[:, :], T.zb[:, :], "zb", BIG, "pd1")
    const(T.keep[:, 0:SL:CAPP], T.keep[:, 0:SL:CAPP], "keep1", 0, "keep")
    const(T.tokw[:, :], T.tokv[:, :], "tokv", -1, "tokm")
    OZ = ["offz", "xq"]
    v("copy", T.xh[:, SL:SL + 32].bitcast(u32), xq.indirect(T.offz[:, :]), reads=OZ, writes=["xhz"], part=True)
    v("copy", T.xhs[:, SL:SL + 32], xs.indirect(T.offz[:, :]), reads=OZ, writes=["xhz"], part=True)
    v("set", T.r2t[:, 4 * N:512], 0.0, writes=["r2z"])
    v("set", T.ns[:, :], 0.0, writes=["ns"])
    v("ts", T.mlt[:, :], T.ecol[:, :], float(me), None, A.is_lt, reads=["ecol"], writes=["mlt"])
    v("qz", T.r2q[:, :], T.r2s[:, :], T.r2t[:, :], reads=["r2t", "r2z"], writes=["r2q"])
    v("tt", T.mcol[:, :], T.ecol[:, :], T.mlt[:, :], A.add, reads=["ecol", "mlt"], writes=["mcol"])
    v("set", T.ht[:, 1024:1032], 0.0, writes=["htz"])
    v("set", T.D2[:, :, SL:SL + 2], 0.0, writes=["D2z"])
    v("qz", T.r8q[:, :], T.r8s[:, :], T.r8t[:, :], reads=["r8t"], writes=["r8q"])
    v("qz", T.wq[:, :], T.ws[:, :], T.wt[:, :], reads=["wt"], writes=["wq"])
    lands("tokl", "at")
    dma("s", "tl", T.tokr[0:1, :], T.tokl[:, 0:CAPP, 0], reads=["tokl"], writes=["tokr"])
    dma("s", "vx", T.vxt[:, :], T.vx[:, :], writes=["vxt"])
    dma("s", "vh", T.vht[:, :], T.vh[:, :], writes=["vht"])

    P = [[T.p1, T.p2, T.p3, T.p4], [T.p0, T.p5, T.p6, T.p7]]
    B = [["p1", "p2", "p3", "p4"], ["p0", "p5", "p6", "p7"]]
    ROW, rw, PE, pe = [T.p1, T.p0], ["p1", "p0"], [T.p2, T.p5], ["p2", "p5"]

    def made(h):
        for i in range(4):
            mm(P[h][i][:, 0:128], T.wq[:, half[i]], T.ws[:, half[i]], T.xh[:, half[h]], T.xhs[:, half[h]], True, True,
               reads=["wq", "xh", "x%d" % h], writes=[B[h][i]])

    def casts(h):
        for i in range(4):
            o = T.ht[:, 512 * h + i:512 * (h + 1):4]
            if i == 3:
                v("ts", o, P[h][i][:, 0:128], 0.0, 0.0625, A.max, A.mult, reads=[B[h][i]], writes=["ht%d" % h], part=True)
            else:
                act(o, P[h][i][:, 0:128], F.Relu, reads=[B[h][i]], writes=["ht%d" % h], part=True, scale=0.0625)

    def pack(h):
        k = slice(HO + 128 * h, XW if h else HO + 128)
        v("qz", T.xh[:, k], T.xhs[:, k], T.ht[:, 512 * h:512 * (h + 1) + 8 * h], reads=["ht%d" % h, "htz"], writes=["h%d" % h])

    def products(h):
        k = slice(HO + 128 * h, HO + 128 * h + 128)
        mm(ROW[h][:, 0:128], T.r8q[:, :], T.r8s[:, :], T.xh[:, k], T.xhs[:, k], True, True, reads=["r8q", "h%d" % h], writes=[rw[h]])
        mm(PE[h][:, 0:128], T.xh[:, k], T.xhs[:, k], T.r2q[:, :], T.r2s[:, :], True, True, reads=["r2q", "h%d" % h], writes=[pe[h]])

    def pens(h):
        v("scan", T.pen[:, half[h]], T.keep[:, half[h]], T.pd[:, half[h]], 0.0, A.mult, A.add, reads=["keep", "pd"], writes=["pen%d" % h])

    def second(h):
        k = 9 * h
        v("scan", T.Rm[:, k + 1:k + 9], T.lim8[:, :], PE[h][:, 0:8], -9e29, A.min, A.max, reads=[pe[h], "lim8"], writes=["Rm%d" % h])

    def away(h):
        v("tt", T.E1[:, half[h]], ROW[h][:, 0:128], T.pen[:, half[h]], A.max, reads=[rw[h], "pen%d" % h], writes=["E1"], part=True)

    def number(h):
        k = 9 * h
        act(T.mj[:, 8 * h:8 * h + 8], T.Rm[:, k:k + 8], F.Sign, reads=["Rm%d" % h, "Rmc"], writes=["mm%d" % h],
            bias=T.Rm[:, k + 7:k + 8], scale=-1.0, accum_out=T.mm[:, h:h + 1])
        act(T.mp[:, h:h + 1], T.mm[:, h:h + 1], F.Copy, reads=["mm%d" % h], writes=["mp%d" % h])
    v("ts", T.feq[0:8, :], T.frl[0:8, :], float(me), -BIG, A.is_equal, A.mult, reads=["frl"], writes=["feq"])
    v("scan", T.ns[0:8, 0:128], T.feq[0:8, :], T.zb[0:8, 0:128], 0.5 * BIG, A.add, A.add, reads=["feq", "zb"], writes=["ns"])
    v("tr", T.nt[:, :], T.ns[:, 127:159], reads=["ns"], writes=["nt"])
    gp("all", T.pd[:, 0:SL:CAPP], T.nt[0:1, 0:N], 128, reads=["nt", "pd1"], writes=["pd"])
    made(hs[0])
    made(hs[1])
    casts(hs[0])
    pack(hs[0])
    products(hs[0])
    casts(hs[1])
    pens(hs[0])
    for a in range(4):
        act(T.Rm[blk[a], 0:18:9], T.pd[blk[a], 32 * a:SL:128], F.Identity, reads=["pd", "ccol"], writes=["Rmc"], part=True,
            bias=T.ccol[blk[a], 0:1])
    pack(hs[1])
    products(hs[1])
    second(hs[0])
    pens(hs[1])
    away(hs[0])
    number(hs[0])
    away(hs[1])
    second(hs[1])
    for h in hs:
        e8 = T.Rm[:, 9 * h + 8:9 * h + 9]
        act(T.SJ[:, row[h]], T.E1[:, :], F.Sign, reads=["E1", "Rm%d" % h], writes=["sg%d" % h],
            bias=e8, scale=-1.0, accum_out=T.sg[:, h:h + 1])
        v("ts", T.EQ[:, row[h]], T.E1[:, :], e8, None, A.is_equal, reads=["E1", "Rm%d" % h], writes=["EQ%d" % h])
    number(hs[1])

    for h in hs:
        v("scan", T.FS[:, row[h]], T.sgn[:, 128 - 128 * h:384 - 128 * h], T.EQ[:, row[h]], T.sg[:, h:h + 1], A.mult, A.add,
          reads=["sgn", "sgn1", "EQ%d" % h, "sg%d" % h], writes=["FS%d" % h])
    for h in hs:
        v("ts", T.fb2[:, blk[h]], T.c128[:, :], T.FS[:, SL * h + SL - 1:SL * h + SL], T.mp[:, h:h + 1], A.is_lt, A.mult,
          reads=["c128", "FS%d" % h, "mp%d" % h], writes=["fb2"], part=True)
    part = [slice(0, 64), slice(64, 128)]
    for a in range(4):
        v("tr", T.fr2[0:32, :, blk[a]], T.fb2[blk[a], :], reads=["fb2"], writes=["fr2%d" % (a // 2)], part=True)
    for k in range(2):
        act(T.fr2[blk[3], :, part[k]], T.fr2[0:32, :, part[k]], F.Copy, reads=["fr2%d" % k], writes=["fr2c%d" % k])
        for b in range(1, 3):
            v("copy", T.fr2[blk[b], :, part[k]], T.fr2[0:32, :, part[k]], reads=["fr2%d" % k], writes=["fr2a%d" % k], part=True)
    for k in range(2):
        for u in range(2):
            v("ts", T.M2[:, 2 * u:2 * u + 2, part[k]], T.fr2[:, :, part[k]], T.mcol[:, u:u + 1], -K, A.is_equal, A.mult,
              reads=["fr2%d" % k, "fr2a%d" % k, "fr2c%d" % k, "mcol"], writes=["M2%d" % u], part=True)
    for s in range(N):
        act(T.tokw[0:1, blk[s]], T.tokr[0:1, blk[s]], F.Identity, reads=["tokr", "tokm"], writes=["tokw"], part=True, bias=float(TK * s))
    for h in range(2):
        for u in range(2):
            v("scan", T.D2[:, u, half[h]], T.M2[:, 2 * u + h, :], T.zb[:, 0:128], T.D2[:, u, 127:128] if h else T.thk[:, 2:3], A.add, A.add,
              reads=["zb", "thk", "M2%d" % u] + ["D2%d" % u] * h, writes=["D2%d" % u], part=True)
    for u in range(2):
        v("scan", T.S2[:, u, 0:SL + 1], T.D2[:, u, 0:SL + 1], T.tokv[:, 1:SL + 2], 0.0, A.max, A.min,
          reads=["tokv", "D2z", "D2%d" % u], writes=["S2%d" % u])
    for b, u in [(2, 0), (3, 0), (2, 1)]:
        act(T.lf2[0:32, 4 * b + 2 * u:4 * b + 2 * u + 2], T.hoc[blk[b], 0:2], F.Identity, reads=["S2%d" % u, "hoc"], writes=["lf2"], part=True,
            bias=T.S2[blk[b], u, SL:SL + 1])
    for b in range(2):
        v("tt", T.lf2[0:32, 4 * b:4 * b + 4], T.S2[blk[b], :, SL - 1:SL + 1], T.hoc[blk[b], :], A.add, reads=["S20", "S21", "hoc"], writes=["lf2"], part=True)
    v("copy", T.offw[0:32, 0:7], T.lf2[0:32, 0:14:2], reads=["lf2"], writes=["offw"])
    act(T.wr[:, :], T.tokw[:, :].indirect(T.offw[:, :]), F.Copy, reads=["offw", "tokw", "tokm"], writes=["wr"])
    for b in range(4):
        v("copy", T.off2[blk[b], :], T.lf2[0:32, 0:14], reads=["lf2"], writes=["off2"], part=True)
    XR = ["off2", "xh", "x0", "x1", "xhz", "h0", "h1"]
    for w in range(2):
        v("copy", T.s2q[:, cols[2][w]].bitcast(u32), T.xh[:, 0:XW].bitcast(u32).indirect(T.off2[:, offs[2][w]]), reads=XR, writes=["q2%d" % w])
        act(T.s2s[:, cols[2][w]], T.xhs[:, 0:XW].indirect(T.off2[:, offs[2][w]]), F.Copy, reads=XR, writes=["s2%d" % w])
    columns(T.s2q, T.s2s, T.l2q, T.l2s, lambda d: blk[come[d].index(me)], CALLS2, ["q20", "s20", "s21", "q21"], ["a20", "a20", "a2s", "a21"])
    for k in "0s1":
        lands("l2" + k, "a2" + k)

    dma("s", "wd", T.whod[:, 0:CB, 0], T.wr[0:1, :], reads=["wr"], writes=["whod"])
    send(others, 2, "aw", lambda d: T.whod[order.index(d)], lambda d: T.whol[me], ["whod"])
    for a in range(N):
        v("ts", T.offh[:, a:a + 1], T.p15[:, 0:1], float(32 * come[me].index(a) + CB), None, A.add, reads=["p15"], writes=["offh"], part=True)
    v("copy", T.l2q[:, blk[n1]].bitcast(u32), xq.indirect(T.offz[:, :]), reads=OZ, writes=["l2z"], part=True)
    act(T.l2s[:, blk[n1]], xs.indirect(T.offz[:, :]), F.Copy, reads=OZ, writes=["l2z"], part=True)
    v("qz", T.vxq[:, :], T.vxs[:, :], T.vxt[:, :], reads=["vxt"], writes=["vxq"])
    v("qz", T.vhq[:, :], T.vhs[:, :], T.vht[:, :], reads=["vht"], writes=["vhq"])
    const(T.ysb[:, CB * me:CB * me + CB], T.zb[:, 0:CB], "zb", 0, "ysb", True)

    act(T.hs[:, :], T.l2s[:, :].indirect(T.offh[:, :]), F.Copy, reads=["l2z", "l20", "l2s", "offh"], writes=["hs"])
    for k in range(4):
        dma("sa"[k % 2], "o%d" % k, T.osc[4 * k:4 * k + 4, :], T.hs[32 * k:32 * k + 4, :], reads=["hs"], writes=["osc%d" % k])
    Y, yt = [T.p0, T.p5], ["p0", "p5"]
    for q in range(2):
        n, t, got = (144, 128)[q], yt[q], ["l2z", "l20"] + ["l2s", "l21"] * q
        k, j = slice(112 * q, 112 * q + n), slice(112 * q + CB, 112 * q + CB + n)
        mm(Y[q][:, 0:n], T.vxq[:, :], T.vxs[:, :], T.l2q[:, k], T.l2s[:, k], True, False, reads=["vxq"] + got, writes=[t])
        mm(Y[q][:, 0:n], T.vhq[:, :], T.vhs[:, :], T.l2q[:, j], T.l2s[:, j], False, True, reads=["vhq"] + got, writes=[t], part=True)
    for c in range(N):
        a, k = come[me][c], 32 * c - 112 * (c > n1)
        if c == n1:
            v("copy", T.hq[:, :].bitcast(u32), T.l2q[:, :].bitcast(u32).indirect(T.offh[:, :]), reads=["l2z", "l20", "l21", "offh"], writes=["hq"])
        else:
            v("copy", T.ysb[:, CB * a:CB * a + CB], Y[c > n1][:, k:k + CB], reads=[yt[c > n1]], writes=["ysb"], part=True)
    dma("a", "oc", T.oc[:, :], T.hq[:, :].bitcast(u8), reads=["hq"], writes=["oc"])
    dma("s", "y", T.y[:, :], T.ysb[:, :], reads=["ysb"], writes=["y"])
    lands("whol", "aw")
    dma("a", "who", T.who[0:1, :], T.whol[:, 0:CB, 0], reads=["whol"], writes=["who"])
    for sem in sorted(cnt):
        if max(seen[q].get(sem, 0) for q in eng) < cnt[sem]:
            need(queue.get(sem, "g"), [(sem, cnt[sem])])
